import numpy as np, ml_dtypes
CORES = [5,29,101,125,133,157,229,253]
N = 8
import mx_ref
BF = ml_dtypes.bfloat16
def cols(t, e):
    v = np.concatenate([t.reshape(128, -1, 4), np.zeros((128, 1, 4), BF)], axis=1)
    return np.ascontiguousarray(v[:, e]).reshape(128, -1)
def decode(q):
    o = []
    for b in range(4):
        e = np.zeros((128, 128, 4), np.float32); e[np.arange(128), np.arange(128), b] = 1
        o.append(mx_ref.matmul(mx_ref.quantize(e.reshape(128, 512).astype(BF)), q))
    return np.stack(o, axis=2).reshape(128, -1)
def f(rng, *shape):
    return mx_ref.flush((rng.standard_normal(shape, dtype=np.float32) * np.exp2(rng.integers(-2, 3, shape[:-1] + (1,)))).astype(BF))
def wide(rng, *shape, cols=0):
    v = rng.standard_normal(shape, dtype=np.float32) * np.exp2(rng.integers(-12, 13, shape)).astype(np.float32)
    if cols: v *= np.repeat(np.exp2(rng.integers(-cols, cols + 1, shape[:-2] + (1, shape[-1] // 4))) * (rng.random(shape[:-2] + (1, shape[-1] // 4)) > 0.0625), 4, axis=-1).astype(np.float32)
    return mx_ref.flush(v.astype(BF))
K = 384
def plant(t, k, v):
    o = t.astype(np.float32).reshape(128, -1, 4); o[:, k] = v
    return o.reshape(128, -1).astype(BF)
def setup_inputs(rng):
    return {"x": f(rng, N, 128, 512), "c1": f(rng, N, 128, 4 * K), "c2": f(rng, N, 128, 4 * K)}
def setup_inputs_last(rng):
    d = setup_inputs(rng); u = f(rng, 128, 4).astype(np.float32).reshape(128, 1, 4); x = []
    s = np.exp2(np.where(np.arange(128) < 120, 2, 0) + np.arange(128) % 2).astype(np.float32).reshape(1, 128, 1)
    for r in range(N):
        x.append(plant(d["x"][r], rng.permutation(128), u * s))
    d["x"] = np.stack(x)
    for c in ("c1", "c2"):
        d[c] = np.stack([plant(d[c][q], [K - 1], np.float32(2) * u) if q == N - 1 else d[c][q] for q in range(N)])
    return d
def setup_inputs_negative(rng):
    d = setup_inputs(rng)
    for c, s in (("x", 1), ("c1", -1), ("c2", -1)):
        d[c] = (np.abs(d[c].astype(np.float32)) * np.float32(s * 2.0 ** 20)).astype(BF)
    return d
def setup_inputs_own(rng):
    d = setup_inputs(rng)
    for c, s in (("c1", 2), ("c2", -2)):
        d[c] = np.stack([plant(d[c][r], rng.permutation(K)[:128], np.float32(s) * d["x"][r].astype(np.float32).reshape(128, -1, 4)) for r in range(N)])
    return d
def setup_inputs_spread(rng):
    d = setup_inputs(rng); d["x"] = wide(rng, N, 128, 512, cols=8)
    for c in ("c1", "c2"): d[c] = wide(rng, N, 128, 4 * K, cols=2)
    return d
def setup_inputs_ties(rng):
    d = setup_inputs(rng)
    d["x"] = np.stack([plant(d["x"][r], rng.permutation(128)[:1], np.zeros((128, 1, 4), np.float32)) for r in range(N)])
    for c in ("c1", "c2"):
        a = f(rng, N, 128, K)
        d[c] = np.stack([cols(np.concatenate([a[q], a[q], a[(q + 1) % N], a[(q + 2) % N]], axis=1), rng.permutation(K)) for q in range(N)])
    return d
def check_inputs(d):
    b = []
    for c in ("x", "c1", "c2"):
        a = np.abs(d[c].astype(np.float32))
        if not (np.isfinite(a) & ((a == 0) | ((a >= 2.0 ** -30) & (a <= 2.0 ** 30)))).all(): b.append(c)
    return b
def winners(v, book):
    s = np.concatenate([mx_ref.matmul(v, q) for q in book], axis=1)
    w = np.argmax(s + np.float32(0), axis=1)
    return w, s[np.arange(128), w]
def chosen(t, e):
    return t.reshape(128, -1, 4)[:, e].reshape(128, -1)
def reference(x, c1, c2):
    q1 = [mx_ref.quantize(c1[q]) for q in range(N)]
    q2 = [mx_ref.quantize(c2[q]) for q in range(N)]
    d1 = np.concatenate([decode(q) for q in q1], axis=1)
    d2 = np.concatenate([decode(q) for q in q2], axis=1)
    y = np.zeros((N, 128, 512), np.float32); no = np.zeros((N, 4, 128), np.float32)
    for r in range(N):
        w1, s1 = winners(mx_ref.quantize(x[r]), q1)
        R = (x[r].astype(np.float32) - chosen(d1, w1)).astype(BF)
        w2, s2 = winners(mx_ref.quantize(R), q2)
        y[r] = R.astype(np.float32) - chosen(d2, w2)
        no[r, 0] = w1; no[r, 1] = w2; no[r, 2] = s1; no[r, 3] = s2
    return {"y": y, "no": no}

@@ -1,0 +1,367 @@
+from concourse.bass import DstId, RemoteDMATransfer
+from concourse.mybir import dt, AluOpType, AxisListType, ActivationFunctionType
+
+N = 8
+K = 384
+BIG = -1.0e29
+F8 = "float8_e4m3fn_x4"
+SCRATCH = {
+    "xb": ("sbuf", [128, 512], "bfloat16"), "c1b": ("sbuf", [128, 4 * K], "bfloat16"), "c2b": ("sbuf", [128, 4 * K], "bfloat16"),
+    "c1d": ("sbuf", [128, 4 * K], "bfloat16"), "eb": ("sbuf", [128, 2048], "bfloat16"), "h": ("sbuf", [128, 8 * 512], "bfloat16"),
+    "rb": ("sbuf", [128, 512], "bfloat16"),
+    "xq": ("sbuf", [128, 128], F8), "xp": ("sbuf", [128, 128], "uint8"),
+    "xrq": ("sbuf", [128, 128], F8), "xrp": ("sbuf", [128, 128], "uint8"),
+    "xsq": ("sbuf", [128, 384], F8), "xsp": ("sbuf", [128, 384], "uint8"),
+    "c1q": ("sbuf", [128, K], F8), "c1p": ("sbuf", [128, K], "uint8"),
+    "c1sq": ("sbuf", [128, K], F8), "c1sp": ("sbuf", [128, K], "uint8"),
+    "c2q": ("sbuf", [128, N * K], F8), "c2p": ("sbuf", [128, N * K], "uint8"),
+    "c2sq": ("sbuf", [128, 192], F8), "c2sp": ("sbuf", [128, 192], "uint8"),
+    "eq": ("sbuf", [128, 512], F8), "ep": ("sbuf", [128, 512], "uint8"),
+    "hq": ("sbuf", [128, 1024], F8), "hp": ("sbuf", [128, 1024], "uint8"),
+    "crq": ("sbuf", [128, 256], F8), "crp": ("sbuf", [128, 256], "uint8"),
+    "cdq": ("sbuf", [128, 1024], F8), "cdp": ("sbuf", [128, 1024], "uint8"),
+    "rq": ("sbuf", [128, 128], F8), "rp": ("sbuf", [128, 128], "uint8"),
+    "ew": ("sbuf", [128, 512], "int32"), "mw": ("sbuf", [128, 32], "int32"), "mw2": ("sbuf", [128, 32], "int32"),
+    "mask": ("sbuf", [128, 32], "float32"), "rst": ("sbuf", [128, 32], "float32"), "neg": ("sbuf", [128, 512], "float32"),
+    "pidx": ("sbuf", [128, 8], "float32"),
+    "m": ("sbuf", [128, 3 * K], "float32"), "junk": ("sbuf", [128, 3 * K], "bfloat16"), "val": ("sbuf", [128, 16], "float32"),
+    "lb": ("sbuf", [128, 160], "float32"), "lt": ("sbuf", [128, 160], "float32"), "ls": ("sbuf", [128, 160], "float32"),
+    "lo": ("sbuf", [128, 40], "uint16"), "sbo": ("sbuf", [128, 16], "float32"),
+    "lst": ("sbuf", [128, 64], "uint16"), "sb": ("sbuf", [128, 32], "float32"),
+    "sel": ("sbuf", [128, 64], "float32"),
+    "dw1": ("sbuf", [128, 4 * 1024], "bfloat16"), "dw2": ("sbuf", [128, 4 * N * K], "bfloat16"),
+    "m2": ("sbuf", [128, N * K], "float32"), "junk2": ("sbuf", [128, N * K], "bfloat16"),
+    "cnt": ("sbuf", [128, 32], "float32"), "tmp": ("sbuf", [128, 512], "float32"), "yo": ("sbuf", [128, 512], "float32"),
+    "ps": ("psum", [128, 4096], "float32"),
+}
+SEMAPHORES = (["cv", "cs", "ct", "cg", "dx", "dc1", "dc2", "dout", "lsem", "xr", "c1s", "c2b", "sbs"]
+              + ["xs%d" % i for i in range(3)] + ["cr%d" % i for i in range(2)]
+              + ["l%d" % i for i in range(8)] + ["cd%d" % i for i in range(8)] + ["c2a%d" % i for i in range(8)])
+MUL, ADD, MAX, MIN = AluOpType.mult, AluOpType.add, AluOpType.max, AluOpType.min
+COPY, SIGN = ActivationFunctionType.Copy, ActivationFunctionType.Sign
+
+
+def bits(engines):
+    return sum(1 << e for e in engines)
+
+
+def rank_program(g, core, T, topo):
+    cores = list(T.cores)
+    home = [c for c in topo.cores_of(core) if T.rank_of(c) is not None]
+    if not home:
+        return
+    rc = home[0]
+    me = T.rank_of(rc)
+
+    def same(a, b):
+        return a == b or topo.same_plane(cores[a], cores[b])
+
+    def pos(a):
+        return [b for b in range(N) if same(a, b)].index(a)
+
+    def cross(a):
+        return [b for b in range(N) if not same(a, b)]
+
+    def roles(a):
+        c = cores[a]
+        far = cores[cross(a)[0]]
+        ports = [p for p in topo.cores_of(c) if p != c and topo.may_write(p, far)]
+        near = [p for p in ports if topo.die(p) == topo.die(c)]
+        away = [p for p in ports if topo.die(p) != topo.die(c)]
+        rest = [p for p in topo.cores_of(c) if p != c and p not in ports]
+        return [near[0], away[0]], [near[1], away[1]], rest
+
+    def kx(a, b):
+        return (pos(a) + pos(b)) % 4
+
+    def delta(a, b):
+        return (pos(a) - pos(b)) % 4
+
+    def place(a, b):
+        return 4 + delta(b, a) if same(a, b) else kx(a, b)
+
+    X = sorted(cross(me), key=lambda b: kx(me, b))
+    Y = {delta(b, me): b for b in range(N) if b != me and same(b, me)}
+    S, B, W = roles(me)
+    likecore = cores[Y[1]]
+
+    eng = {"v": g.vector, "s": g.scalar, "t": g.tensor, "g": g, "y": g.sync}
+    cnt = {"v": 0, "s": 0, "t": 0, "g": 0}
+    seen = {}
+    tot = {}
+
+    def need(q, deps):
+        best = {}
+        for s, n in deps:
+            best[s] = max(best.get(s, 0), n)
+        for s in best:
+            if seen.get((q, s), 0) < best[s]:
+                eng[q].wait_ge(T.sem[s], best[s])
+                seen[(q, s)] = best[s]
+
+    def do(q, deps, fn):
+        need(q, deps)
+        i = fn(eng[q])
+        cnt[q] += 1
+        i.then_inc(T.sem["c" + q], 1)
+        return ("c" + q, cnt[q])
+
+    def load(q, sem, out, in_, deps=()):
+        need(q, deps)
+        eng[q].dma_start(out, in_).then_inc(T.sem[sem], 16)
+        tot[sem] = tot.get(sem, 0) + 16
+        return (sem, tot[sem])
+
+    def send(deps, transfers):
+        need("g", deps)
+        out = []
+        for engines, src, dsts, sem in transfers:
+            ids = []
+            for c, _ in dsts:
+                rid, pid = topo.addr(c, core)
+                ids.append(DstId(rid=rid, pnc=pid))
+            out.append(RemoteDMATransfer(dst_ids=ids, dma_engine_mask=bits(engines), remote_sem=T.sem[sem], srcs=[src], dsts=[d for _, d in dsts]))
+            tot["lsem"] = tot.get("lsem", 0) + len(engines)
+        g.remote_dma_fused(out, local_sem=T.sem["lsem"])
+
+    def c8(t, a, b):
+        return t[:, a:b].bitcast(dt.uint8)
+
+    def send_tiles(deps, items):
+        send(deps, [(e, c8(q, a, b), [(c, c8(dq, z, z + b - a)) for c, dq, dp, z in ds], sem) for e, q, p, a, b, ds, sem in items])
+        send(deps, [(e, p[:, a:b], [(c, dp[:, z:z + b - a]) for c, dq, dp, z in ds], sem) for e, q, p, a, b, ds, sem in items])
+
+    def finish():
+        need("g", [("c" + q, n) for q, n in cnt.items() if n] + [(s, n) for s, n in tot.items()])
+
+    off = topo.engines(core, likecore)
+    onchip = topo.engines(core, [c for c in topo.cores_of(core) if c != core][0])
+    high = [e for e in onchip if e not in off]
+
+    if core in B or core in W:
+        if core in B:
+            n, at, dests, arr = 192, 192 * B.index(core), X, 2 * len(off)
+        else:
+            n, at, dests, arr = 128, 128 * W.index(core), [Y[d] for d in Y], 2 * (len(onchip) // 4)
+        col = me * K + at
+        send_tiles([("c2b", arr)], [(off, T.c2sq, T.c2sp, 0, n, [(cores[b], T.c2q, T.c2p, col) for b in dests], "c2a%d" % me)])
+        finish()
+        return
+
+    k_mw = do("g", [], lambda e: e.iota(T.mw[:, :], [[-1, 32]], 128, 1))
+    k_neg = do("v", [], lambda e: e.memset(T.neg[:, :], BIG))
+    k_r = do("v", [], lambda e: e.memset(T.rst[:, :], 1.0))
+    k_r = do("v", [k_r], lambda e: e.memset(T.rst[:, 0:1], 0.0))
+    k_r = do("v", [k_r], lambda e: e.memset(T.rst[:, 16:17], 0.0))
+    k_m = do("v", [k_mw], lambda e: e.tensor_scalar(T.mw2[:, :], T.mw[:, :], 15, None, AluOpType.bitwise_and))
+    k_m = do("v", [k_m], lambda e: e.tensor_scalar(T.mask[:, :], T.mw2[:, :], 0.0, None, AluOpType.is_equal))
+
+    banks = {"n": 0, "free": [[] for _ in range(8)]}
+
+    def product(deps, lq, lp, a, rq, rp, b, n):
+        i = banks["n"] % 8
+        banks["n"] += 1
+        o = T.ps[:, 512 * i:512 * i + n]
+        t = do("t", list(deps) + banks["free"][i], lambda e: e.matmul_mx(o, lq[:, a:a + 128], lp[:, a:a + 128], rq[:, b:b + n], rp[:, b:b + n], True, True))
+        return i, t
+
+    def build_list(val, deps, i, dst, d):
+        f = slice(32 * i, 32 * i + 32)
+        t = do("v", list(deps) + [k_m], lambda e: e.tensor_scalar(T.lb[:, f], T.mask[:, :], val, None, MUL))
+        t = do("v", [t], lambda e: e.transpose(T.lt[:, f], T.lb[:, f]))
+        t = do("v", [t, k_r], lambda e: e.tensor_tensor_scan(T.ls[:, f], T.rst[:, :], T.lt[:, f], 0.0, MUL, ADD))
+        for a in range(4):
+            u = do("v", [t], lambda e: e.tensor_copy(dst[0:32, d + 2 * a:d + 2 * a + 2], T.ls[32 * a:32 * a + 32, 32 * i + 15:32 * i + 32:16]))
+        u = do("v", [u], lambda e: e.tensor_copy(dst[32:64, d:d + 8], dst[0:32, d:d + 8]))
+        return do("v", [u], lambda e: e.tensor_copy(dst[64:128, d:d + 8], dst[0:64, d:d + 8]))
+
+    def score(deps, xq, xp, a, cq, cp, i):
+        b, t = product(deps, xq, xp, a, cq, cp, 0, K)
+        m = T.m[:, K * i:K * i + K]
+        ts = do("v", [t, k_neg], lambda e: e.tensor_tensor_scan(m, T.ps[:, 512 * b:512 * b + K], T.neg[:, 0:K], BIG, MAX, MAX))
+        banks["free"][b] = [ts]
+        tv = do("s", [ts], lambda e: e.activation(T.junk[:, K * i:K * i + K], m, SIGN, bias=T.m[:, K * i + K - 1:K * i + K], scale=-1.0, accum_out=T.val[:, 4 * i:4 * i + 1]))
+        return ts, tv
+
+    def tell(i, ts, tv, dst, d):
+        do("v", [ts], lambda e: e.tensor_copy(dst[:, d:d + 1], T.m[:, K * i + K - 1:K * i + K]))
+        return do("v", [tv], lambda e: e.tensor_scalar(dst[:, d + 1:d + 2], T.val[:, 4 * i:4 * i + 1], float(me * K), None, ADD))
+
+    if core in S:
+        s = S.index(core)
+        owners = [X[2 * s], X[2 * s + 1], Y[s + 1]]
+        e4 = len(off) // 2
+        send_tiles([("xr", 2 * len(high))], [(off[e4 * i:e4 * i + e4], T.xrq, T.xrp, 0, 128, [(roles(owners[i])[0][s], T.xsq, T.xsp, 128 * i)], "xs%d" % i) for i in range(2)])
+        arr = [2 * e4, 2 * e4, 2 * len(off)]
+        c1 = ("c1s", 2 * len(onchip))
+        st = {}
+        for i in (0, 1):
+            st[i] = score([c1, ("xs%d" % i, arr[i])], T.xsq, T.xsp, 128 * i, T.c1sq, T.c1sp, i)
+        for i in (0, 1, 2):
+            if i == 2:
+                st[i] = score([c1, ("xs2", arr[2])], T.xsq, T.xsp, 256, T.c1sq, T.c1sp, 2)
+            b = owners[i]
+            tl = build_list(T.val[:, 4 * i:4 * i + 1], [st[i][1]], i, T.lo, 8 * i)
+            send([tl], [(off, T.lo[:, 8 * i:8 * i + 8], [(rc, T.lst[:, 8 * b:8 * b + 8])], "l%d" % b)])
+            tb = tell(i, st[i][0], st[i][1], T.sbo, 4 * i)
+            p = 4 * place(b, me)
+            send([tb], [(off, T.sbo[:, 4 * i:4 * i + 2], [(cores[b], T.sb[:, p:p + 2])], "sbs")])
+        for i in (0, 1):
+            b = owners[i]
+            p = place(b, me)
+            send_tiles([("cr%d" % i, 2 * len(off))], [(off, T.crq, T.crp, 128 * i, 128 * i + 128, [(cores[b], T.cdq, T.cdp, 128 * p)], "cd%d" % p)])
+        finish()
+        return
+
+    l_x = load("y", "dx", T.xb[:, :], T.x[:, :])
+    l_1 = load("s", "dc1", T.c1b[:, :], T.c1[:, :])
+    l_2 = load("s", "dc2", T.c2b[:, :], T.c2[:, :])
+    k_w = do("g", [], lambda e: e.iota(T.ew[:, :], [[1, 512]], 0, -4))
+    k_p = do("g", [], lambda e: e.iota(T.pidx[:, :], [[128, 8]], 0, 1, allow_small_or_imprecise_dtypes=True))
+    q_x = do("v", [l_x], lambda e: e.quantize_mx(T.xq[:, :], T.xp[:, :], T.xb[:, :]))
+    like = [roles(b)[0][delta(me, b) - 1] if delta(me, b) < 3 else cores[b] for b in Y.values()]
+    send_tiles([q_x], [(high, T.xq, T.xp, 0, 128, [(c, T.xrq, T.xrp, 0) for c in S], "xr"),
+                       (off, T.xq, T.xp, 0, 128, [(c, T.xsq, T.xsp, 256) for c in like], "xs2")])
+    q_1 = do("v", [l_1], lambda e: e.quantize_mx(T.c1q[:, :], T.c1p[:, :], T.c1b[:, :]))
+    send_tiles([q_1], [(onchip, T.c1q, T.c1p, 0, K, [(c, T.c1sq, T.c1sp, 0) for c in S], "c1s")])
+    for t in range(4):
+        k_d = do("s", [l_1], lambda e: e.activation(T.c1d[:, K * t:K * t + K], T.c1b[:, t:4 * K:4], COPY))
+    for t in range(4):
+        k_e = do("v", [k_w], lambda e: e.tensor_scalar(T.eb[:, 512 * t:512 * t + 512], T.ew[:, :], float(t), None, AluOpType.is_equal))
+    k_e = do("v", [k_e], lambda e: e.quantize_mx(T.eq[:, :], T.ep[:, :], T.eb[:, :]))
+    o2 = me * K
+    q_2 = do("v", [l_2], lambda e: e.quantize_mx(T.c2q[:, o2:o2 + K], T.c2p[:, o2:o2 + K], T.c2b[:, :]))
+    send_tiles([q_2], [(e, T.c2q, T.c2p, o2 + 192 * i, o2 + 192 * i + 192, [(B[i], T.c2sq, T.c2sp, 0)], "c2b") for i, e in enumerate([high, off])])
+    w4 = len(onchip) // 4
+    send_tiles([q_2], [(onchip[w4 * i:w4 * i + w4], T.c2q, T.c2p, o2 + 128 * i, o2 + 128 * i + 128, [(W[i], T.c2sq, T.c2sp, 0)], "c2b") for i in range(3)])
+
+    s_own = score([q_x, q_1], T.xq, T.xp, 0, T.c1q, T.c1p, 0)
+    s_3 = score([q_1, ("xs2", 2 * len(off))], T.xsq, T.xsp, 256, T.c1q, T.c1p, 1)
+    t_own = build_list(T.val[:, 0:1], [s_own[1]], 0, T.lo, 0)
+    t_sb = tell(0, s_own[0], s_own[1], T.sb, 16)
+    t_3 = build_list(T.val[:, 4:5], [s_3[1]], 1, T.lo, 8)
+    t_sb3 = tell(1, s_3[0], s_3[1], T.sbo, 4)
+
+    def gather(q, lst, a, deps, i):
+        for t in range(4):
+            o = T.h[:, 512 * i + t:512 * i + 512:4]
+            w = T.c1d[:, K * t:K * t + K].indirect(lst[:, a:a + 8])
+            if q == "v":
+                k = do("v", list(deps) + [k_d], lambda e: e.tensor_copy(o, w))
+            else:
+                k = do("s", list(deps) + [k_d], lambda e: e.activation(o, w, COPY))
+        return k
+
+    ga = gather("s", T.lo, 8, [t_3], 6)
+    gb = gather("v", T.lo, 0, [t_own], 7)
+    q_own = do("v", [gb], lambda e: e.quantize_mx(T.cdq[:, 512:640], T.cdp[:, 512:640], T.h[:, 7 * 512:8 * 512]))
+    q_3 = do("v", [ga], lambda e: e.quantize_mx(T.hq[:, 768:896], T.hp[:, 768:896], T.h[:, 6 * 512:7 * 512]))
+    b = Y[3]
+    p = place(b, me)
+    send([t_sb3], [(off, T.sbo[:, 4:6], [(cores[b], T.sb[:, 4 * p:4 * p + 2])], "sbs")])
+    send_tiles([q_3], [(off, T.hq, T.hp, 768, 896, [(cores[b], T.cdq, T.cdp, 128 * p)], "cd%d" % p)])
+
+    NK = N * K
+    k_w2 = []
+
+    def decode2(owner, deps):
+        for t in range(4):
+            i, k = product(list(deps) + [k_e, q_2], T.eq, T.ep, 128 * t, T.c2q, T.c2p, owner * K, K)
+            o = T.dw2[:, NK * t + owner * K:NK * t + owner * K + K]
+            src = T.ps[:, 512 * i:512 * i + K]
+            if t % 2 == 0:
+                r = do("v", [k], lambda e: e.tensor_scalar(o, src, -1.0, None, MUL))
+            else:
+                r = do("s", [k], lambda e: e.activation(o, src, COPY, scale=-1.0))
+            banks["free"][i] = [r]
+            k_w2.append(r)
+
+    decode2(me, [])
+    for i in range(2):
+        r0, r1 = X[i], X[2 + i]
+        ga = gather("v", T.lst, 8 * r0, [("l%d" % r0, len(off))], 2 * i)
+        gb = gather("s", T.lst, 8 * r1, [("l%d" % r1, len(off))], 2 * i + 1)
+        z = 256 * i
+        q = do("v", [ga, gb], lambda e: e.quantize_mx(T.hq[:, z:z + 256], T.hp[:, z:z + 256], T.h[:, 4 * z:4 * z + 1024]))
+        send_tiles([q], [(e, T.hq, T.hp, z + 128 * j, z + 128 * j + 128, [(S[j], T.crq, T.crp, 128 * i)], "cr%d" % i) for j, e in enumerate([high, off])])
+    r0, r1 = Y[1], Y[2]
+    ga = gather("v", T.lst, 8 * r0, [("l%d" % r0, len(off))], 4)
+    gb = gather("s", T.lst, 8 * r1, [("l%d" % r1, len(off))], 5)
+    q = do("v", [ga, gb], lambda e: e.quantize_mx(T.hq[:, 512:768], T.hp[:, 512:768], T.h[:, 2048:3072]))
+    e4 = len(off) // 2
+    send_tiles([q], [(off[e4 * j:e4 * j + e4], T.hq, T.hp, 512 + 128 * j, 640 + 128 * j, [(cores[r], T.cdq, T.cdp, 128 * place(r, me))], "cd%d" % place(r, me)) for j, r in enumerate([r0, r1])])
+
+    for d in (1, 2, 3):
+        decode2(Y[d], [("c2a%d" % Y[d], 3 * 2 * len(off))])
+
+    sel = T.sel
+    sc, nu = T.sb[:, 0:32:4], T.sb[:, 1:32:4]
+    k = do("v", [t_sb, ("sbs", 7 * len(off))], lambda e: e.tensor_reduce(sel[:, 0:1], sc, AxisListType.X, MAX))
+    k = do("v", [k], lambda e: e.tensor_scalar(sel[:, 8:16], sc, sel[:, 0:1], 16384.0, AluOpType.is_lt, MUL))
+    k = do("v", [k], lambda e: e.tensor_tensor(sel[:, 16:24], sel[:, 8:16], nu, ADD))
+    k_n = do("v", [k], lambda e: e.tensor_reduce(sel[:, 1:2], sel[:, 16:24], AxisListType.X, MIN))
+    k = do("v", [k_n], lambda e: e.tensor_scalar(sel[:, 24:32], nu, sel[:, 1:2], None, AluOpType.is_equal))
+    k = do("v", [k, k_p], lambda e: e.tensor_tensor(sel[:, 32:40], sel[:, 24:32], T.pidx[:, :], MUL))
+    k = do("v", [k], lambda e: e.tensor_reduce(sel[:, 2:3], sel[:, 32:40], AxisListType.X, ADD))
+    k_l1 = build_list(sel[:, 2:3], [k], 2, T.lo, 16)
+    load("y", "dout", T.no[0:1, :], sel[:, 1:2], [k_n])
+    load("y", "dout", T.no[2:3, :], sel[:, 0:1], [k_n])
+
+    for b in X:
+        decode2(b, [("c2a%d" % b, 2 * 2 * len(off))])
+
+    k_w1 = []
+
+    def decode1(z, deps):
+        for t in range(4):
+            i, k = product(list(deps) + [k_e], T.eq, T.ep, 128 * t, T.cdq, T.cdp, z, 512)
+            o = T.dw1[:, 1024 * t + z:1024 * t + z + 512]
+            src = T.ps[:, 512 * i:512 * i + 512]
+            if t % 2 == 0:
+                r = do("v", [k], lambda e: e.tensor_scalar(o, src, -1.0, None, MUL))
+            else:
+                r = do("s", [k], lambda e: e.activation(o, src, COPY, scale=-1.0))
+            banks["free"][i] = [r]
+            k_w1.append(r)
+
+    dl = []
+    for b in Y.values():
+        dl.append(("cd%d" % place(me, b), 2 * len(off) if delta(me, b) == 3 else len(off)))
+    decode1(512, [q_own] + dl)
+    decode1(0, [("cd%d" % p, 2 * len(off)) for p in range(4)])
+
+    def winners(win, width, lst, a, deps, base, out):
+        ks = {}
+        for t in (2, 3):
+            w = win[:, width * t:width * t + width].indirect(lst[:, a:a + 8])
+            ks[t] = do("s", deps, lambda e: e.activation(T.tmp[:, 128 * t:128 * t + 128], w, COPY))
+        for t in (0, 1):
+            w = win[:, width * t:width * t + width].indirect(lst[:, a:a + 8])
+            k = do("v", deps, lambda e: e.tensor_tensor(out[:, t:512:4], w, base[:, t:512:4], ADD))
+        for t in (2, 3):
+            k = do("v", [ks[t]], lambda e: e.tensor_tensor(out[:, t:512:4], T.tmp[:, 128 * t:128 * t + 128], base[:, t:512:4], ADD))
+        return k
+
+    k_r1 = winners(T.dw1, 1024, T.lo, 16, [k_l1] + k_w1, T.xb, T.rb)
+    q_r = do("v", [k_r1], lambda e: e.quantize_mx(T.rq[:, :], T.rp[:, :], T.rb[:, :]))
+
+    n2 = NK // 512
+    last = []
+    cn = []
+    for i in range(n2):
+        b, k = product([q_r], T.rq, T.rp, 0, T.c2q, T.c2p, 512 * i, 512)
+        z = 512 * i
+        ini = BIG if i == 0 else T.m2[:, z - 1:z]
+        k = do("v", [k] + last, lambda e: e.tensor_tensor_scan(T.m2[:, z:z + 512], T.ps[:, 512 * b:512 * b + 512], T.neg[:, :], ini, MAX, MAX))
+        banks["free"][b] = [k]
+        last = [k]
+        cn.append(do("s", [k], lambda e: e.activation(T.junk2[:, z:z + 512], T.m2[:, z:z + 512], SIGN, bias=T.m2[:, z + 511:z + 512], scale=-1.0, accum_out=T.cnt[:, i:i + 1])))
+    load("y", "dout", T.no[3:4, :], T.m2[:, NK - 1:NK], last)
+    k = do("v", last, lambda e: e.tensor_scalar(T.cnt[:, 8:8 + n2], T.m2[:, 511:NK:512], T.m2[:, NK - 1:NK], 512.0, AluOpType.is_lt, MUL))
+    k = do("v", [k] + cn, lambda e: e.tensor_tensor(T.cnt[:, 16:16 + n2], T.cnt[:, 8:8 + n2], T.cnt[:, 0:n2], MAX))
+    k = do("v", [k], lambda e: e.tensor_reduce(T.cnt[:, 24:25], T.cnt[:, 16:16 + n2], AxisListType.X, ADD))
+    load("y", "dout", T.no[1:2, :], T.cnt[:, 24:25], [k])
+    k = build_list(T.cnt[:, 24:25], [k], 3, T.lo, 24)
+    k = winners(T.dw2, NK, T.lo, 24, [k] + k_w2, T.rb, T.yo)
+    load("y", "dout", T.y[:, :], T.yo[:, :], [k])
+    finish()

@@ -3,11 +3,13 @@ from concourse.mybir import dt, AluOpType, AxisListType, ActivationFunctionType
 
 N = 8
 K = 384
+WORLD = 256
 BIG = -1.0e29
 F8 = "float8_e4m3fn_x4"
+O = dict(load="21", plan="xl21", fwd=0, car="dr", late=2, early=1, ld=(1, 2), fd=(0,), bx=(1,), h0=192, fw4=0, cut=28, dram=0, mid=0)
 SCRATCH = {
     "xb": ("sbuf", [128, 512], "bfloat16"), "c1b": ("sbuf", [128, 4 * K], "bfloat16"), "c2b": ("sbuf", [128, 4 * K], "bfloat16"),
-    "c1d": ("sbuf", [128, 4 * K], "bfloat16"), "eb": ("sbuf", [128, 2048], "bfloat16"), "h": ("sbuf", [128, 8 * 512], "bfloat16"),
+    "ew": ("sbuf", [128, 528], "bfloat16"), "eb": ("sbuf", [128, 528], "bfloat16"), "h": ("sbuf", [128, 8 * 512], "bfloat16"),
     "rb": ("sbuf", [128, 512], "bfloat16"),
     "xq": ("sbuf", [128, 128], F8), "xp": ("sbuf", [128, 128], "uint8"),
     "xrq": ("sbuf", [128, 128], F8), "xrp": ("sbuf", [128, 128], "uint8"),
@@ -15,28 +17,33 @@ SCRATCH = {
     "c1q": ("sbuf", [128, K], F8), "c1p": ("sbuf", [128, K], "uint8"),
     "c1sq": ("sbuf", [128, K], F8), "c1sp": ("sbuf", [128, K], "uint8"),
     "c2q": ("sbuf", [128, N * K], F8), "c2p": ("sbuf", [128, N * K], "uint8"),
-    "c2sq": ("sbuf", [128, 192], F8), "c2sp": ("sbuf", [128, 192], "uint8"),
     "eq": ("sbuf", [128, 512], F8), "ep": ("sbuf", [128, 512], "uint8"),
     "hq": ("sbuf", [128, 1024], F8), "hp": ("sbuf", [128, 1024], "uint8"),
     "crq": ("sbuf", [128, 256], F8), "crp": ("sbuf", [128, 256], "uint8"),
     "cdq": ("sbuf", [128, 1024], F8), "cdp": ("sbuf", [128, 1024], "uint8"),
     "rq": ("sbuf", [128, 128], F8), "rp": ("sbuf", [128, 128], "uint8"),
-    "ew": ("sbuf", [128, 512], "int32"), "mw": ("sbuf", [128, 32], "int32"), "mw2": ("sbuf", [128, 32], "int32"),
-    "mask": ("sbuf", [128, 32], "float32"), "rst": ("sbuf", [128, 32], "float32"), "neg": ("sbuf", [128, 512], "float32"),
-    "pidx": ("sbuf", [128, 8], "float32"),
+    "mw": ("sbuf", [128, 32], "int32"), "mw2": ("sbuf", [128, 32], "int32"), "mt": ("sbuf", [128, 32], "float32"),
+    "mask": ("sbuf", [128, 32], "float32"), "rst": ("sbuf", [128, 96], "float32"), "neg": ("sbuf", [128, 512], "bfloat16"),
+    "pi": ("sbuf", [128, 8], "int32"), "pidx": ("sbuf", [128, 8], "float32"), "pj": ("sbuf", [128, 8], "float32"),
     "m": ("sbuf", [128, 3 * K], "float32"), "junk": ("sbuf", [128, 3 * K], "bfloat16"), "val": ("sbuf", [128, 16], "float32"),
     "lb": ("sbuf", [128, 160], "float32"), "lt": ("sbuf", [128, 160], "float32"), "ls": ("sbuf", [128, 160], "float32"),
-    "lo": ("sbuf", [128, 40], "uint16"), "sbo": ("sbuf", [128, 16], "float32"),
-    "lst": ("sbuf", [128, 64], "uint16"), "sb": ("sbuf", [128, 32], "float32"),
+    "lo": ("sbuf", [128, 160], "uint16"), "sbo": ("sbuf", [128, 16], "float32"),
+    "lst": ("sbuf", [128, 160], "uint16"), "sb": ("sbuf", [128, 32], "float32"),
     "sel": ("sbuf", [128, 64], "float32"),
     "dw1": ("sbuf", [128, 4 * 1024], "bfloat16"), "dw2": ("sbuf", [128, 4 * N * K], "bfloat16"),
     "m2": ("sbuf", [128, N * K], "float32"), "junk2": ("sbuf", [128, N * K], "bfloat16"),
-    "cnt": ("sbuf", [128, 32], "float32"), "tmp": ("sbuf", [128, 512], "float32"), "yo": ("sbuf", [128, 512], "float32"),
+    "cnt": ("sbuf", [128, 32], "float32"), "yo": ("sbuf", [128, 512], "float32"),
     "ps": ("psum", [128, 4096], "float32"),
 }
-SEMAPHORES = (["cv", "cs", "ct", "cg", "dx", "dc1", "dc2", "dout", "lsem", "xr", "c1s", "c2b", "sbs"]
-              + ["xs%d" % i for i in range(3)] + ["cr%d" % i for i in range(2)]
-              + ["l%d" % i for i in range(8)] + ["cd%d" % i for i in range(8)] + ["c2a%d" % i for i in range(8)])
+WID = [O["h0"], K - O["h0"]]
+for _h in range(2):
+    for _j in range(3):
+        SCRATCH["bq%d%d" % (_h, _j)] = ("dram" if O["dram"] else "sbuf", [128, WID[_h]], F8)
+        SCRATCH["bp%d%d" % (_h, _j)] = ("dram" if O["dram"] else "sbuf", [128, WID[_h]], "uint8")
+SEMAPHORES = (["cv", "cs", "ct", "cg", "dx", "dc1", "dc2", "dout", "lsem", "xr", "xrp", "c1s", "c1sp", "c2b", "c2bp", "sbs"]
+              + ["xs%d" % i for i in range(3)] + ["cr%d" % i for i in range(2)] + ["crp%d" % i for i in range(2)]
+              + ["mr%d" % i for i in range(4)] + ["mrp%d" % i for i in range(4)]
+              + ["l%d" % i for i in range(3)] + ["cd%d" % i for i in range(8)] + ["c2a%d" % i for i in range(8)])
 MUL, ADD, MAX, MIN = AluOpType.mult, AluOpType.add, AluOpType.max, AluOpType.min
 COPY, SIGN = ActivationFunctionType.Copy, ActivationFunctionType.Sign
 
@@ -47,11 +54,11 @@ def bits(engines):
 
 def rank_program(g, core, T, topo):
     cores = list(T.cores)
-    home = [c for c in topo.cores_of(core) if T.rank_of(c) is not None]
+    home = [a for a in range(N) if cores[a] in topo.cores_of(core) or topo.mates(core, cores[a])]
     if not home:
         return
-    rc = home[0]
-    me = T.rank_of(rc)
+    me = home[0]
+    rc = cores[me]
 
     def same(a, b):
         return a == b or topo.same_plane(cores[a], cores[b])
@@ -59,17 +66,14 @@ def rank_program(g, core, T, topo):
     def pos(a):
         return [b for b in range(N) if same(a, b)].index(a)
 
-    def cross(a):
-        return [b for b in range(N) if not same(a, b)]
-
     def roles(a):
         c = cores[a]
-        far = cores[cross(a)[0]]
-        ports = [p for p in topo.cores_of(c) if p != c and topo.may_write(p, far)]
-        near = [p for p in ports if topo.die(p) == topo.die(c)]
-        away = [p for p in ports if topo.die(p) != topo.die(c)]
-        rest = [p for p in topo.cores_of(c) if p != c and p not in ports]
-        return [near[0], away[0]], [near[1], away[1]], rest
+        mate = [p for p in range(WORLD) if topo.mates(c, p)]
+        near = lambda ps: sorted(ps, key=lambda p: topo.die(p) != topo.die(c))
+        ports = near([p for p in topo.cores_of(c) if topo.may_write(p, mate[0])])
+        rest = near([p for p in topo.cores_of(c) if p != c and p not in ports])
+        back = near([p for p in mate if topo.may_write(p, c)])
+        return ports[0::2], ports[1::2], rest[0:2], [back[0:2], back[2:4]]
 
     def kx(a, b):
         return (pos(a) + pos(b)) % 4
@@ -78,12 +82,29 @@ def rank_program(g, core, T, topo):
         return (pos(a) - pos(b)) % 4
 
     def place(a, b):
-        return 4 + delta(b, a) if same(a, b) else kx(a, b)
+        return {3: 4, 1: 5, 2: 6, 0: 7}[delta(a, b)] if same(a, b) else kx(a, b)
 
-    X = sorted(cross(me), key=lambda b: kx(me, b))
+    def direct(a, b):
+        return delta(a, b) in O["ld"] if same(a, b) else kx(a, b) in O["fd"]
+
+    def road(a, b):
+        return (direct(a, b) == (O["car"] == "rd"), delta(a, b) if same(a, b) else kx(a, b), same(a, b))
+
+    def relayed(b):
+        return sorted([a for a in range(N) if a != b and not direct(a, b)], key=lambda a: (turn(a, b), same(a, b)))
+
+    def by_w(a, b):
+        return same(a, b) == direct(a, b) and (same(a, b) or kx(a, b) not in O["bx"])
+
+    def carried(a, w):
+        return sorted([b for b in range(N) if b != a and by_w(a, b) == w], key=lambda b: road(a, b))
+
+    def turn(a, b):
+        return carried(a, by_w(a, b)).index(b)
+
+    X = sorted([b for b in range(N) if not same(me, b)], key=lambda b: kx(me, b))
     Y = {delta(b, me): b for b in range(N) if b != me and same(b, me)}
-    S, B, W = roles(me)
-    likecore = cores[Y[1]]
+    S, B, W, M = roles(me)
 
     eng = {"v": g.vector, "s": g.scalar, "t": g.tensor, "g": g, "y": g.sync}
     cnt = {"v": 0, "s": 0, "t": 0, "g": 0}
@@ -127,34 +148,64 @@ def rank_program(g, core, T, topo):
     def c8(t, a, b):
         return t[:, a:b].bitcast(dt.uint8)
 
-    def send_tiles(deps, items):
-        send(deps, [(e, c8(q, a, b), [(c, c8(dq, z, z + b - a)) for c, dq, dp, z in ds], sem) for e, q, p, a, b, ds, sem in items])
-        send(deps, [(e, p[:, a:b], [(c, dp[:, z:z + b - a]) for c, dq, dp, z in ds], sem) for e, q, p, a, b, ds, sem in items])
+    def send_tiles(dq, dp, items):
+        send(dq, [(e, c8(q, a, a + n), [(c, c8(oq, z, z + n)) for c, oq, op, z in ds], sq) for e, q, p, a, n, ds, sq, sp in items])
+        send(dp, [(e, p[:, a:a + n], [(c, op[:, z:z + n]) for c, oq, op, z in ds], sp) for e, q, p, a, n, ds, sq, sp in items])
 
     def finish():
         need("g", [("c" + q, n) for q, n in cnt.items() if n] + [(s, n) for s, n in tot.items()])
 
-    off = topo.engines(core, likecore)
+    def share(engines, n):
+        w = len(engines) // n
+        return [engines[w * i:w * i + w] for i in range(n)]
+
+    off = topo.engines(core, cores[Y[1]] if core in topo.cores_of(rc) else roles(Y[1])[3][0][0])
     onchip = topo.engines(core, [c for c in topo.cores_of(core) if c != core][0])
     high = [e for e in onchip if e not in off]
+    NO, Q4 = len(off), len(onchip) // 4
+    halves = share(off, 2)
+
+    def slot(h, j):
+        return T["bq%d%d" % (h, j)], T["bp%d%d" % (h, j)]
+
+    def x_out(k, e):
+        return (e, T.xrq, T.xrp, 0, 128, [(roles(X[k])[0][k // 2], T.xsq, T.xsp, 128 * (k % 2))], "xs%d" % (k % 2), "xs%d" % (k % 2))
 
     if core in B or core in W:
-        if core in B:
-            n, at, dests, arr = 192, 192 * B.index(core), X, 2 * len(off)
-        else:
-            n, at, dests, arr = 128, 128 * W.index(core), [Y[d] for d in Y], 2 * (len(onchip) // 4)
-        col = me * K + at
-        send_tiles([("c2b", arr)], [(off, T.c2sq, T.c2sp, 0, n, [(cores[b], T.c2q, T.c2p, col) for b in dests], "c2a%d" % me)])
+        h = (B if core in B else W).index(core)
+        if O["fw4"] and core in B:
+            send_tiles([("xr", NO)], [("xrp", NO)], [x_out(2 * h + 1, off)])
+        q, p = slot(h, 0)
+        dq, dp = [("c2b", O.get("nb", Q4))], [("c2bp", O.get("nb", Q4))]
+        for b in carried(me, core in W):
+            if direct(me, b):
+                send_tiles(dq, dp, [(off, q, p, 0, WID[h], [(cores[b], T.c2q, T.c2p, me * K + WID[0] * h)], "c2a%d" % me, "c2a%d" % me)])
+            else:
+                i = relayed(b).index(me)
+                send_tiles(dq, dp, [(off, q, p, 0, WID[h], [(roles(b)[3][h][i % 2],) + slot(h, i // 2) + (0,)], "mr%d" % (i // 2), "mrp%d" % (i // 2))])
         finish()
         return
+    if core in M[0] + M[1]:
+        h = int(core in M[1])
+        for i, a in enumerate(relayed(me)):
+            if M[h][i % 2] == core:
+                j = i // 2
+                q, p = slot(h, j)
+                send_tiles([("mr%d" % j, NO)], [("mrp%d" % j, NO)], [(off, q, p, 0, WID[h], [(rc, T.c2q, T.c2p, a * K + WID[0] * h)], "c2a%d" % a, "c2a%d" % a)])
+        finish()
+        return
+    if core != rc and core not in S:
+        return
 
-    k_mw = do("g", [], lambda e: e.iota(T.mw[:, :], [[-1, 32]], 128, 1))
+    k_a = do("g", [], lambda e: e.iota(T.mw[:, :], [[0, 2], [-1, 4], [0, 4]], 128, 1))
+    k_b = do("g", [], lambda e: e.iota(T.mt[:, :], [[0, 8], [1, 4]], 0, 0, allow_small_or_imprecise_dtypes=True))
     k_neg = do("v", [], lambda e: e.memset(T.neg[:, :], BIG))
     k_r = do("v", [], lambda e: e.memset(T.rst[:, :], 1.0))
-    k_r = do("v", [k_r], lambda e: e.memset(T.rst[:, 0:1], 0.0))
-    k_r = do("v", [k_r], lambda e: e.memset(T.rst[:, 16:17], 0.0))
-    k_m = do("v", [k_mw], lambda e: e.tensor_scalar(T.mw2[:, :], T.mw[:, :], 15, None, AluOpType.bitwise_and))
-    k_m = do("v", [k_m], lambda e: e.tensor_scalar(T.mask[:, :], T.mw2[:, :], 0.0, None, AluOpType.is_equal))
+    k_r = do("v", [k_r], lambda e: e.memset(T.rst[:, 0:96:4], 0.0))
+    k_m = do("v", [k_a], lambda e: e.tensor_scalar(T.mw2[:, :], T.mw[:, :], 3, None, AluOpType.bitwise_and))
+    k_m = do("v", [k_m], lambda e: e.tensor_scalar(T.lb[:, 0:32], T.mw2[:, :], 0.0, -65536.0, AluOpType.not_equal, MUL))
+    k_b = do("v", [k_b], lambda e: e.tensor_scalar(T.lt[:, 0:32], T.mt[:, :], 0.25, None, MUL))
+    k_m = do("v", [k_m, k_b], lambda e: e.tensor_tensor(T.mask[:, :], T.lb[:, 0:32], T.lt[:, 0:32], ADD))
 
     banks = {"n": 0, "free": [[] for _ in range(8)]}
 
@@ -165,15 +216,17 @@ def rank_program(g, core, T, topo):
         t = do("t", list(deps) + banks["free"][i], lambda e: e.matmul_mx(o, lq[:, a:a + 128], lp[:, a:a + 128], rq[:, b:b + n], rp[:, b:b + n], True, True))
         return i, t
 
-    def build_list(val, deps, i, dst, d):
-        f = slice(32 * i, 32 * i + 32)
-        t = do("v", list(deps) + [k_m], lambda e: e.tensor_scalar(T.lb[:, f], T.mask[:, :], val, None, MUL))
-        t = do("v", [t], lambda e: e.transpose(T.lt[:, f], T.lb[:, f]))
-        t = do("v", [t, k_r], lambda e: e.tensor_tensor_scan(T.ls[:, f], T.rst[:, :], T.lt[:, f], 0.0, MUL, ADD))
+    def build_lists(vals, deps, z, turned, mask=T.mask):
+        n = 32 * len(vals)
+        for i, v in enumerate(vals):
+            t = do("v", list(deps[i]) + [k_m], lambda e: e.tensor_scalar(T.lb[:, z + 32 * i:z + 32 * i + 32], mask[:, :], v, 0.0, ADD, MAX))
+        t = do("v", [t], lambda e: e.transpose(T.lt[:, z:z + n], T.lb[:, z:z + n]))
+        t = do("v", [t, k_r], lambda e: e.tensor_tensor_scan(T.ls[:, z:z + n], T.rst[:, 0:n], T.lt[:, z:z + n], 0.0, MUL, ADD))
         for a in range(4):
-            u = do("v", [t], lambda e: e.tensor_copy(dst[0:32, d + 2 * a:d + 2 * a + 2], T.ls[32 * a:32 * a + 32, 32 * i + 15:32 * i + 32:16]))
-        u = do("v", [u], lambda e: e.tensor_copy(dst[32:64, d:d + 8], dst[0:32, d:d + 8]))
-        return do("v", [u], lambda e: e.tensor_copy(dst[64:128, d:d + 8], dst[0:64, d:d + 8]))
+            o = T.lo[0:32, z + a:z + n:4] if turned else T.lo[0:32, z + 8 * a:z + 8 * a + 8]
+            u = do("v", [t], lambda e: e.tensor_scalar(o, T.ls[32 * a:32 * a + 32, z + 3:z + n:4], 4.0, None, MUL))
+        u = do("v", [u], lambda e: e.tensor_copy(T.lo[32:64, z:z + n], T.lo[0:32, z:z + n]))
+        return do("v", [u], lambda e: e.tensor_copy(T.lo[64:128, z:z + n], T.lo[0:64, z:z + n]))
 
     def score(deps, xq, xp, a, cq, cp, i):
         b, t = product(deps, xq, xp, a, cq, cp, 0, K)
@@ -183,173 +236,181 @@ def rank_program(g, core, T, topo):
         tv = do("s", [ts], lambda e: e.activation(T.junk[:, K * i:K * i + K], m, SIGN, bias=T.m[:, K * i + K - 1:K * i + K], scale=-1.0, accum_out=T.val[:, 4 * i:4 * i + 1]))
         return ts, tv
 
-    def tell(i, ts, tv, dst, d):
-        do("v", [ts], lambda e: e.tensor_copy(dst[:, d:d + 1], T.m[:, K * i + K - 1:K * i + K]))
-        return do("v", [tv], lambda e: e.tensor_scalar(dst[:, d + 1:d + 2], T.val[:, 4 * i:4 * i + 1], float(me * K), None, ADD))
+    def tell(i, st, dst, d):
+        do("s", [st[0]], lambda e: e.activation(dst[:, d:d + 1], T.m[:, K * i + K - 1:K * i + K], COPY))
+        return do("s", [st[1]], lambda e: e.activation(dst[:, d + 1:d + 2], T.val[:, 4 * i:4 * i + 1], COPY, bias=float(me * K)))
+
+    def claim(b, i, e):
+        p = 4 * place(b, me)
+        return (e, T.sbo[:, 4 * i:4 * i + 2], [(cores[b], T.sb[:, p:p + 2])], "sbs")
+
+    val = lambda i: T.val[:, 4 * i:4 * i + 1]
 
     if core in S:
         s = S.index(core)
-        owners = [X[2 * s], X[2 * s + 1], Y[s + 1]]
-        e4 = len(off) // 2
-        send_tiles([("xr", 2 * len(high))], [(off[e4 * i:e4 * i + e4], T.xrq, T.xrp, 0, 128, [(roles(owners[i])[0][s], T.xsq, T.xsp, 128 * i)], "xs%d" % i) for i in range(2)])
-        arr = [2 * e4, 2 * e4, 2 * len(off)]
-        c1 = ("c1s", 2 * len(onchip))
-        st = {}
-        for i in (0, 1):
-            st[i] = score([c1, ("xs%d" % i, arr[i])], T.xsq, T.xsp, 128 * i, T.c1sq, T.c1sp, i)
-        for i in (0, 1, 2):
-            if i == 2:
-                st[i] = score([c1, ("xs2", arr[2])], T.xsq, T.xsp, 256, T.c1sq, T.c1sp, 2)
-            b = owners[i]
-            tl = build_list(T.val[:, 4 * i:4 * i + 1], [st[i][1]], i, T.lo, 8 * i)
-            send([tl], [(off, T.lo[:, 8 * i:8 * i + 8], [(rc, T.lst[:, 8 * b:8 * b + 8])], "l%d" % b)])
-            tb = tell(i, st[i][0], st[i][1], T.sbo, 4 * i)
-            p = 4 * place(b, me)
-            send([tb], [(off, T.sbo[:, 4 * i:4 * i + 2], [(cores[b], T.sb[:, p:p + 2])], "sbs")])
-        for i in (0, 1):
-            b = owners[i]
+        owners = [X[2 * s], X[2 * s + 1]]
+        if O["fw4"]:
+            send_tiles([("xr", NO)], [("xrp", NO)], [x_out(2 * s, off)])
+        else:
+            send_tiles([("xr", NO)], [("xrp", NO)], [x_out(2 * s + i, halves[i]) for i in range(2)])
+        if O["fwd"] and s == 0:
+            send_tiles([("c1s", NO)], [("c1sp", NO)], [(high, T.c1sq, T.c1sp, 0, K, [(S[1], T.c1sq, T.c1sp, 0)], "c1s", "c1sp")])
+        c1 = [("c1s", NO), ("c1sp", NO)]
+        st = [score(c1 + [("xs%d" % i, NO * (1 + O["fw4"]))], T.xsq, T.xsp, 128 * i, T.c1sq, T.c1sp, i) for i in range(2)]
+        tl = build_lists([val(0), val(1)], [[st[0][1]], [st[1][1]]], 0, True)
+        send([tl], [(off, T.lo[:, 0:64], [(rc, T.lst[:, 64 * s:64 * s + 64])], "l%d" % s)])
+        tb = [tell(i, st[i], T.sbo, 4 * i) for i in range(2)]
+        send(tb, [claim(owners[i], i, halves[i]) for i in range(2)])
+        if s == O.get("s3", 1):
+            s3 = score([("xs2", 2 * NO)], T.xsq, T.xsp, 256, T.c1sq, T.c1sp, 2)
+            tl = build_lists([val(2)], [[s3[1]]], 64, True)
+            send([tl], [(off, T.lo[:, 64:96], [(rc, T.lst[:, 128:160])], "l2")])
+            tb = tell(2, s3, T.sbo, 8)
+            send([tb], [claim(Y[3], 2, off)])
+        for i in range(2):
+            b = X[2 * i + s]
             p = place(b, me)
-            send_tiles([("cr%d" % i, 2 * len(off))], [(off, T.crq, T.crp, 128 * i, 128 * i + 128, [(cores[b], T.cdq, T.cdp, 128 * p)], "cd%d" % p)])
+            send_tiles([("cr%d" % i, NO)], [("crp%d" % i, NO)], [(off, T.crq, T.crp, 128 * i, 128, [(cores[b], T.cdq, T.cdp, 128 * p)], "cd%d" % p, "cd%d" % p)])
         finish()
         return
 
     l_x = load("y", "dx", T.xb[:, :], T.x[:, :])
-    l_1 = load("s", "dc1", T.c1b[:, :], T.c1[:, :])
-    l_2 = load("s", "dc2", T.c2b[:, :], T.c2[:, :])
-    k_w = do("g", [], lambda e: e.iota(T.ew[:, :], [[1, 512]], 0, -4))
-    k_p = do("g", [], lambda e: e.iota(T.pidx[:, :], [[128, 8]], 0, 1, allow_small_or_imprecise_dtypes=True))
+    for b in O["load"]:
+        if b == "1":
+            l_1 = load("y", "dc1", T.c1b[:, :], T.c1[:, :])
+        else:
+            l_2 = load("y", "dc2", T.c2b[:, :], T.c2[:, :])
+    k_w = do("g", [], lambda e: e.iota(T.ew[:, :], [[1, 528]], -3, -4, allow_small_or_imprecise_dtypes=True))
+    k_p = do("g", [], lambda e: e.iota(T.pi[:, 0:1], [[0, 1]], 0, 1))
+    k_q = do("g", [], lambda e: e.iota(T.pidx[:, :], [[128, 8]], 0, 0, allow_small_or_imprecise_dtypes=True))
+    k_d = do("v", [k_w], lambda e: e.tensor_scalar(T.eb[:, :], T.ew[:, :], 0.0, None, AluOpType.is_equal))
     q_x = do("v", [l_x], lambda e: e.quantize_mx(T.xq[:, :], T.xp[:, :], T.xb[:, :]))
-    like = [roles(b)[0][delta(me, b) - 1] if delta(me, b) < 3 else cores[b] for b in Y.values()]
-    send_tiles([q_x], [(high, T.xq, T.xp, 0, 128, [(c, T.xrq, T.xrp, 0) for c in S], "xr"),
-                       (off, T.xq, T.xp, 0, 128, [(c, T.xsq, T.xsp, 256) for c in like], "xs2")])
-    q_1 = do("v", [l_1], lambda e: e.quantize_mx(T.c1q[:, :], T.c1p[:, :], T.c1b[:, :]))
-    send_tiles([q_1], [(onchip, T.c1q, T.c1p, 0, K, [(c, T.c1sq, T.c1sp, 0) for c in S], "c1s")])
     for t in range(4):
-        k_d = do("s", [l_1], lambda e: e.activation(T.c1d[:, K * t:K * t + K], T.c1b[:, t:4 * K:4], COPY))
-    for t in range(4):
-        k_e = do("v", [k_w], lambda e: e.tensor_scalar(T.eb[:, 512 * t:512 * t + 512], T.ew[:, :], float(t), None, AluOpType.is_equal))
-    k_e = do("v", [k_e], lambda e: e.quantize_mx(T.eq[:, :], T.ep[:, :], T.eb[:, :]))
+        k_e = do("v", [k_d], lambda e: e.quantize_mx(T.eq[:, 128 * t:128 * t + 128], T.ep[:, 128 * t:128 * t + 128], T.eb[:, 3 - t:515 - t]))
+    like = {delta(me, b): b for b in Y.values()}
+    xo = [(cores[like[1]], T.xsq, T.xsp, 0), (cores[like[2]], T.xsq, T.xsp, 128), (roles(like[3])[0][O.get("s3", 1)], T.xsq, T.xsp, 256)]
     o2 = me * K
-    q_2 = do("v", [l_2], lambda e: e.quantize_mx(T.c2q[:, o2:o2 + K], T.c2p[:, o2:o2 + K], T.c2b[:, :]))
-    send_tiles([q_2], [(e, T.c2q, T.c2p, o2 + 192 * i, o2 + 192 * i + 192, [(B[i], T.c2sq, T.c2sp, 0)], "c2b") for i, e in enumerate([high, off])])
-    w4 = len(onchip) // 4
-    send_tiles([q_2], [(onchip[w4 * i:w4 * i + w4], T.c2q, T.c2p, o2 + 128 * i, o2 + 128 * i + 128, [(W[i], T.c2sq, T.c2sp, 0)], "c2b") for i in range(3)])
-
-    s_own = score([q_x, q_1], T.xq, T.xp, 0, T.c1q, T.c1p, 0)
-    s_3 = score([q_1, ("xs2", 2 * len(off))], T.xsq, T.xsp, 256, T.c1q, T.c1p, 1)
-    t_own = build_list(T.val[:, 0:1], [s_own[1]], 0, T.lo, 0)
-    t_sb = tell(0, s_own[0], s_own[1], T.sb, 16)
-    t_3 = build_list(T.val[:, 4:5], [s_3[1]], 1, T.lo, 8)
-    t_sb3 = tell(1, s_3[0], s_3[1], T.sbo, 4)
-
-    def gather(q, lst, a, deps, i):
-        for t in range(4):
-            o = T.h[:, 512 * i + t:512 * i + 512:4]
-            w = T.c1d[:, K * t:K * t + K].indirect(lst[:, a:a + 8])
-            if q == "v":
-                k = do("v", list(deps) + [k_d], lambda e: e.tensor_copy(o, w))
+    for b in O["load"]:
+        if b == "1":
+            q_1 = do("v", [l_1], lambda e: e.quantize_mx(T.c1q[:, :], T.c1p[:, :], T.c1b[:, :]))
+        else:
+            q_2 = do("v", [l_2], lambda e: e.quantize_mx(T.c2q[:, o2:o2 + K], T.c2p[:, o2:o2 + K], T.c2b[:, :]))
+    for step in O["plan"]:
+        if step == "x":
+            send_tiles([q_x], [], [(e, T.xq, T.xp, 0, 128, [(c, T.xrq, T.xrp, 0) for c in cs], "xr", "xrp") for e, cs in [(high, S), (off, B)][:1 + O["fw4"]]])
+        if step == "l":
+            send_tiles([q_x], [], [(off, T.xq, T.xp, 0, 128, xo[:2], "xs0", "xs0")])
+        if step == "2":
+            four = share(high, 2) + share(off, 2)
+            if WID[0] == WID[1]:
+                send_tiles([q_2], [], [(four[i], T.c2q, T.c2p, o2 + WID[0] * (i % 2), WID[0], [((B + W)[i],) + slot(i % 2, 0) + (0,)], "c2b", "c2bp") for i in range(4)])
             else:
-                k = do("s", list(deps) + [k_d], lambda e: e.activation(o, w, COPY))
-        return k
-
-    ga = gather("s", T.lo, 8, [t_3], 6)
-    gb = gather("v", T.lo, 0, [t_own], 7)
-    q_own = do("v", [gb], lambda e: e.quantize_mx(T.cdq[:, 512:640], T.cdp[:, 512:640], T.h[:, 7 * 512:8 * 512]))
-    q_3 = do("v", [ga], lambda e: e.quantize_mx(T.hq[:, 768:896], T.hp[:, 768:896], T.h[:, 6 * 512:7 * 512]))
-    b = Y[3]
-    p = place(b, me)
-    send([t_sb3], [(off, T.sbo[:, 4:6], [(cores[b], T.sb[:, 4 * p:4 * p + 2])], "sbs")])
-    send_tiles([q_3], [(off, T.hq, T.hp, 768, 896, [(cores[b], T.cdq, T.cdp, 128 * p)], "cd%d" % p)])
+                for h in (1, 0):
+                    send_tiles([q_2], [], [(e, T.c2q, T.c2p, o2 + WID[0] * h, WID[h], [(c,) + slot(h, 0) + (0,)], "c2b", "c2bp") for c, e in [(B[h], high), (W[h], off)]])
+        if step in "BW":
+            for h in (1, 0):
+                send_tiles([q_2], [], [(high if step == "B" else off, T.c2q, T.c2p, o2 + WID[0] * h, WID[h], [((B if step == "B" else W)[h],) + slot(h, 0) + (0,)], "c2b", "c2bp")])
+        if step == "1":
+            if O["fwd"]:
+                send_tiles([q_1], [], [(off, T.c1q, T.c1p, 0, K, [(S[0], T.c1sq, T.c1sp, 0)], "c1s", "c1sp")])
+            else:
+                send_tiles([q_1], [], [(e, T.c1q, T.c1p, 0, K, [(c, T.c1sq, T.c1sp, 0)], "c1s", "c1sp") for c, e in zip(S, [off, high])])
+    send_tiles([], [], [(off, T.xq, T.xp, 0, 128, xo[2:], "xs2", "xs2")])
+    k = do("v", [k_p], lambda e: e.tensor_scalar(T.pi[:, 1:2], T.pi[:, 0:1], 5, None, AluOpType.arith_shift_right))
+    k = do("v", [k_p], lambda e: e.tensor_scalar(T.pi[:, 2:3], T.pi[:, 0:1], 28, None, AluOpType.bitwise_and))
+    k = do("v", [k_p], lambda e: e.tensor_scalar(T.pi[:, 3:4], T.pi[:, 0:1], 3, None, AluOpType.bitwise_and))
+    k = do("v", [k], lambda e: e.tensor_copy(T.pj[:, 0:3], T.pi[:, 1:4]))
+    k = do("v", [k], lambda e: e.tensor_scalar(T.pj[:, 4:5], T.pj[:, 0:1], T.pj[:, 1:2], 4.0, ADD, MUL))
+    k_p = do("v", [k, k_q], lambda e: e.tensor_scalar(T.pidx[:, :], T.pidx[:, :], T.pj[:, 4:5], T.pj[:, 2:3], ADD, ADD))
 
     NK = N * K
-    k_w2 = []
+    k_w1, k_w2 = [], []
 
-    def decode2(owner, deps):
+    def decode(q, p, z, n, out, deps, done, by="svsv"):
         for t in range(4):
-            i, k = product(list(deps) + [k_e, q_2], T.eq, T.ep, 128 * t, T.c2q, T.c2p, owner * K, K)
-            o = T.dw2[:, NK * t + owner * K:NK * t + owner * K + K]
-            src = T.ps[:, 512 * i:512 * i + K]
-            if t % 2 == 0:
+            i, k = product(list(deps) + [k_e], T.eq, T.ep, 128 * t, q, p, z, n)
+            o = out[:, 4 * z + t:4 * (z + n):4]
+            src = T.ps[:, 512 * i:512 * i + n]
+            if by[t] == "v":
                 r = do("v", [k], lambda e: e.tensor_scalar(o, src, -1.0, None, MUL))
             else:
                 r = do("s", [k], lambda e: e.activation(o, src, COPY, scale=-1.0))
             banks["free"][i] = [r]
-            k_w2.append(r)
+            done.append(r)
 
-    decode2(me, [])
+    def decode2(a, by="svsv"):
+        decode(T.c2q, T.c2p, a * K, K, T.dw2, [("c2a%d" % a, 4 * NO)], k_w2, by)
+
+    def gather(lst, a, n, cut, deps, z):
+        kv = do("v", deps, lambda e: e.tensor_copy(T.h[:, z:z + 16 * cut], T.c1b[:, :].indirect(lst[:, a:a + cut])))
+        ks = do("s", deps, lambda e: e.activation(T.h[:, z + 16 * cut:z + 16 * n], T.c1b[:, :].indirect(lst[:, a + cut:a + n]), COPY))
+        return [kv, ks]
+
+    def back(b, e, z):
+        p = place(b, me)
+        return (e, T.hq, T.hp, z, 128, [(cores[b], T.cdq, T.cdp, 128 * p)], "cd%d" % p, "cd%d" % p)
+
+    st = [score([q_x, q_1], T.xq, T.xp, 0, T.c1q, T.c1p, 0)]
+    tl = build_lists([val(0)], [[st[0][1]]], 64, True)
+    t_sb = tell(0, st[0], T.sb, 28)
+    ga = gather(T.lo, 64, 32, 12, [tl, l_1], 3584)
+    q_own = do("v", ga, lambda e: e.quantize_mx(T.cdq[:, 896:1024], T.cdp[:, 896:1024], T.h[:, 3584:4096]))
+    decode(T.c2q, T.c2p, me * K, K, T.dw2, [q_2], k_w2)
+    st += [score([("xs0", 4 * NO)], T.xsq, T.xsp, 128 * i, T.c1q, T.c1p, 1 + i) for i in range(2)]
+    tl = build_lists([val(1), val(2)], [[st[1][1]], [st[2][1]]], 0, True)
+    tb = [tell(1 + i, st[1 + i], T.sbo, 4 * i) for i in range(2)]
+    send(tb, [claim(Y[1 + i], i, halves[i]) for i in range(2)])
+    ga = gather(T.lo, 0, 64, O["cut"], [tl], 0)
+    q = do("v", ga, lambda e: e.quantize_mx(T.hq[:, 0:256], T.hp[:, 0:256], T.h[:, 0:1024]))
+    send_tiles([q], [], [back(Y[1 + i], halves[i], 128 * i) for i in range(2)])
+
+    far = [a for a in range(N) if a != me]
+    parts = sorted(far, key=lambda a: turn(a, me) + (0 if direct(a, me) else O.get("pen", 1.5)))
+    for a in parts[:O["early"]]:
+        decode2(a)
     for i in range(2):
-        r0, r1 = X[i], X[2 + i]
-        ga = gather("v", T.lst, 8 * r0, [("l%d" % r0, len(off))], 2 * i)
-        gb = gather("s", T.lst, 8 * r1, [("l%d" % r1, len(off))], 2 * i + 1)
-        z = 256 * i
-        q = do("v", [ga, gb], lambda e: e.quantize_mx(T.hq[:, z:z + 256], T.hp[:, z:z + 256], T.h[:, 4 * z:4 * z + 1024]))
-        send_tiles([q], [(e, T.hq, T.hp, z + 128 * j, z + 128 * j + 128, [(S[j], T.crq, T.crp, 128 * i)], "cr%d" % i) for j, e in enumerate([high, off])])
-    r0, r1 = Y[1], Y[2]
-    ga = gather("v", T.lst, 8 * r0, [("l%d" % r0, len(off))], 4)
-    gb = gather("s", T.lst, 8 * r1, [("l%d" % r1, len(off))], 5)
-    q = do("v", [ga, gb], lambda e: e.quantize_mx(T.hq[:, 512:768], T.hp[:, 512:768], T.h[:, 2048:3072]))
-    e4 = len(off) // 2
-    send_tiles([q], [(off[e4 * j:e4 * j + e4], T.hq, T.hp, 512 + 128 * j, 640 + 128 * j, [(cores[r], T.cdq, T.cdp, 128 * place(r, me))], "cd%d" % place(r, me)) for j, r in enumerate([r0, r1])])
+        z = 256 + 256 * i
+        ga = gather(T.lst, 64 * i, 64, O["cut"], [("l%d" % i, NO)], 4 * z)
+        q = do("v", ga, lambda e: e.quantize_mx(T.hq[:, z:z + 256], T.hp[:, z:z + 256], T.h[:, 4 * z:4 * z + 1024]))
+        send_tiles([q], [], [(e, T.hq, T.hp, z + 128 * j, 128, [(S[j], T.crq, T.crp, 128 * i)], "cr%d" % i, "crp%d" % i) for j, e in enumerate([off, high])])
+    ga = gather(T.lst, 128, 32, 12, [("l2", NO)], 3072)
+    q = do("v", ga, lambda e: e.quantize_mx(T.hq[:, 768:896], T.hp[:, 768:896], T.h[:, 3072:3584]))
+    send_tiles([q], [], [back(Y[3], off, 768)])
 
-    for d in (1, 2, 3):
-        decode2(Y[d], [("c2a%d" % Y[d], 3 * 2 * len(off))])
+    decode(T.cdq, T.cdp, 640, 384, T.dw1, [q_own, ("cd5", NO), ("cd6", NO)], k_w1)
 
     sel = T.sel
     sc, nu = T.sb[:, 0:32:4], T.sb[:, 1:32:4]
-    k = do("v", [t_sb, ("sbs", 7 * len(off))], lambda e: e.tensor_reduce(sel[:, 0:1], sc, AxisListType.X, MAX))
+    k = do("v", [t_sb, ("sbs", 4 * NO)], lambda e: e.tensor_reduce(sel[:, 0:1], sc, AxisListType.X, MAX))
     k = do("v", [k], lambda e: e.tensor_scalar(sel[:, 8:16], sc, sel[:, 0:1], 16384.0, AluOpType.is_lt, MUL))
     k = do("v", [k], lambda e: e.tensor_tensor(sel[:, 16:24], sel[:, 8:16], nu, ADD))
     k_n = do("v", [k], lambda e: e.tensor_reduce(sel[:, 1:2], sel[:, 16:24], AxisListType.X, MIN))
     k = do("v", [k_n], lambda e: e.tensor_scalar(sel[:, 24:32], nu, sel[:, 1:2], None, AluOpType.is_equal))
     k = do("v", [k, k_p], lambda e: e.tensor_tensor(sel[:, 32:40], sel[:, 24:32], T.pidx[:, :], MUL))
     k = do("v", [k], lambda e: e.tensor_reduce(sel[:, 2:3], sel[:, 32:40], AxisListType.X, ADD))
-    k_l1 = build_list(sel[:, 2:3], [k], 2, T.lo, 16)
+    k_l1 = build_lists([sel[:, 2:3]], [[k]], 96, False)
     load("y", "dout", T.no[0:1, :], sel[:, 1:2], [k_n])
     load("y", "dout", T.no[2:3, :], sel[:, 0:1], [k_n])
 
-    for b in X:
-        decode2(b, [("c2a%d" % b, 2 * 2 * len(off))])
-
-    k_w1 = []
-
-    def decode1(z, deps):
-        for t in range(4):
-            i, k = product(list(deps) + [k_e], T.eq, T.ep, 128 * t, T.cdq, T.cdp, z, 512)
-            o = T.dw1[:, 1024 * t + z:1024 * t + z + 512]
-            src = T.ps[:, 512 * i:512 * i + 512]
-            if t % 2 == 0:
-                r = do("v", [k], lambda e: e.tensor_scalar(o, src, -1.0, None, MUL))
-            else:
-                r = do("s", [k], lambda e: e.activation(o, src, COPY, scale=-1.0))
-            banks["free"][i] = [r]
-            k_w1.append(r)
-
-    dl = []
-    for b in Y.values():
-        dl.append(("cd%d" % place(me, b), 2 * len(off) if delta(me, b) == 3 else len(off)))
-    decode1(512, [q_own] + dl)
-    decode1(0, [("cd%d" % p, 2 * len(off)) for p in range(4)])
-
-    def winners(win, width, lst, a, deps, base, out):
-        ks = {}
-        for t in (2, 3):
-            w = win[:, width * t:width * t + width].indirect(lst[:, a:a + 8])
-            ks[t] = do("s", deps, lambda e: e.activation(T.tmp[:, 128 * t:128 * t + 128], w, COPY))
-        for t in (0, 1):
-            w = win[:, width * t:width * t + width].indirect(lst[:, a:a + 8])
-            k = do("v", deps, lambda e: e.tensor_tensor(out[:, t:512:4], w, base[:, t:512:4], ADD))
-        for t in (2, 3):
-            k = do("v", [ks[t]], lambda e: e.tensor_tensor(out[:, t:512:4], T.tmp[:, 128 * t:128 * t + 128], base[:, t:512:4], ADD))
-        return k
-
-    k_r1 = winners(T.dw1, 1024, T.lo, 16, [k_l1] + k_w1, T.xb, T.rb)
-    q_r = do("v", [k_r1], lambda e: e.quantize_mx(T.rq[:, :], T.rp[:, :], T.rb[:, :]))
+    nl = len(parts) - O["late"]
+    nm = nl - O["mid"]
+    for a in parts[O["early"]:nm]:
+        decode2(a)
+    decode(T.cdq, T.cdp, 0, 256, T.dw1, [("cd0", 2 * NO), ("cd1", 2 * NO)], k_w1)
+    for a in parts[nm:nl]:
+        decode2(a)
+    for p in (4, 3, 2):
+        decode(T.cdq, T.cdp, 128 * p, 128, T.dw1, [("cd%d" % p, 2 * NO)], k_w1)
+    k = do("v", [k_l1] + k_w1, lambda e: e.tensor_tensor(T.rb[:, :], T.dw1[:, :].indirect(T.lo[:, 96:128]), T.xb[:, :], ADD))
+    q_r = do("v", [k], lambda e: e.quantize_mx(T.rq[:, :], T.rp[:, :], T.rb[:, :]))
+    for a in parts[nl:nl + 1]:
+        decode2(a, "ssss")
 
     n2 = NK // 512
     last = []
     cn = []
     for i in range(n2):
-        b, k = product([q_r], T.rq, T.rp, 0, T.c2q, T.c2p, 512 * i, 512)
+        b, k = product([q_r] + [("c2a%d" % a, 4 * NO) for a in parts], T.rq, T.rp, 0, T.c2q, T.c2p, 512 * i, 512)
         z = 512 * i
         ini = BIG if i == 0 else T.m2[:, z - 1:z]
         k = do("v", [k] + last, lambda e: e.tensor_tensor_scan(T.m2[:, z:z + 512], T.ps[:, 512 * b:512 * b + 512], T.neg[:, :], ini, MAX, MAX))
@@ -357,11 +418,18 @@ def rank_program(g, core, T, topo):
         last = [k]
         cn.append(do("s", [k], lambda e: e.activation(T.junk2[:, z:z + 512], T.m2[:, z:z + 512], SIGN, bias=T.m2[:, z + 511:z + 512], scale=-1.0, accum_out=T.cnt[:, i:i + 1])))
     load("y", "dout", T.no[3:4, :], T.m2[:, NK - 1:NK], last)
-    k = do("v", last, lambda e: e.tensor_scalar(T.cnt[:, 8:8 + n2], T.m2[:, 511:NK:512], T.m2[:, NK - 1:NK], 512.0, AluOpType.is_lt, MUL))
-    k = do("v", [k] + cn, lambda e: e.tensor_tensor(T.cnt[:, 16:16 + n2], T.cnt[:, 8:8 + n2], T.cnt[:, 0:n2], MAX))
-    k = do("v", [k], lambda e: e.tensor_reduce(T.cnt[:, 24:25], T.cnt[:, 16:16 + n2], AxisListType.X, ADD))
-    load("y", "dout", T.no[1:2, :], T.cnt[:, 24:25], [k])
-    k = build_list(T.cnt[:, 24:25], [k], 3, T.lo, 24)
-    k = winners(T.dw2, NK, T.lo, 24, [k] + k_w2, T.rb, T.yo)
-    load("y", "dout", T.y[:, :], T.yo[:, :], [k])
+    n1 = n2 - 1
+    k = do("v", last, lambda e: e.tensor_scalar(T.cnt[:, 8:8 + n1], T.m2[:, 511:NK - 1:512], T.m2[:, NK - 1:NK], 512.0, AluOpType.is_lt, MUL))
+    k = do("v", [k] + cn[:n1], lambda e: e.tensor_tensor(T.cnt[:, 16:16 + n1], T.cnt[:, 8:8 + n1], T.cnt[:, 0:n1], MAX))
+    k_c = do("v", [k], lambda e: e.tensor_reduce(T.cnt[:, 24:25], T.cnt[:, 16:16 + n1], AxisListType.X, ADD))
+    k = do("v", [k_c], lambda e: e.tensor_scalar(T.mt[:, :], T.mask[:, :], T.cnt[:, 24:25], None, ADD))
+    k_n = do("s", [k_c, cn[n1]], lambda e: e.activation(T.cnt[:, 28:29], T.cnt[:, n1:n2], ActivationFunctionType.Identity, bias=T.cnt[:, 24:25]))
+    load("y", "dout", T.no[1:2, :], T.cnt[:, 28:29], [k_n])
+    for a in parts[nl + 1:]:
+        decode2(a, "svss")
+    k = build_lists([T.cnt[:, n1:n2]], [[k, cn[n1]]], 128, False, T.mt)
+    for i, q in enumerate("sy"):
+        f = slice(256 * i, 256 * i + 256)
+        r = do("v", [k] + k_w2, lambda e: e.tensor_tensor(T.yo[:, f], T.dw2[:, :].indirect(T.lo[:, 128 + 16 * i:144 + 16 * i]), T.rb[:, f], ADD))
+        load(q, "dout", T.y[:, f], T.yo[:, f], [r])
     finish()

@@ -6,44 +6,48 @@ K = 384
 WORLD = 256
 BIG = -1.0e29
 F8 = "float8_e4m3fn_x4"
-O = dict(load="21", plan="xl21", fwd=0, car="dr", late=2, early=1, ld=(1, 2), fd=(0,), bx=(1,), h0=192, fw4=0, cut=28, dram=0, mid=0)
+O = dict(load="21", plan="xl2ae", fwd=0, car="dr", late=2, early=1, ld=(1, 2), fd=(0,), bx=(1,), h0=192, fw4=0, dram=2, mid=0,
+         likeearly=0, runs=(128, 384, 512, 512, 512, 512, 512), arb=2, pf="pq", ra=0, g2="BW", S="", B="u0 l1 l2 l3", W="u1 u2 u3", rel1="u1 u3",
+         arr="u0 l1 l2 u1 u2 l3 u3", lk=0, le="off", seq="pppnpa23", l1="v---", l2="-sss", k1="ssss", k0="sv--", l0="v---", cv=0, batch=((1, 2, 3),), via=(1, 2, 3), ahead=(2, 4), sq=1, l1c=0, two=1, help="W0W1S1", rounds=((0, 2), (2, 1), (3, 1)), run=384, je="off")
 SCRATCH = {
     "xb": ("sbuf", [128, 512], "bfloat16"), "c1b": ("sbuf", [128, 4 * K], "bfloat16"), "c2b": ("sbuf", [128, 4 * K], "bfloat16"),
+    "c1d": ("sbuf", [128, 4 * K], "bfloat16"),
     "ew": ("sbuf", [128, 528], "bfloat16"), "eb": ("sbuf", [128, 528], "bfloat16"), "h": ("sbuf", [128, 8 * 512], "bfloat16"),
     "rb": ("sbuf", [128, 512], "bfloat16"),
     "xq": ("sbuf", [128, 128], F8), "xp": ("sbuf", [128, 128], "uint8"),
     "xrq": ("sbuf", [128, 128], F8), "xrp": ("sbuf", [128, 128], "uint8"),
-    "xsq": ("sbuf", [128, 384], F8), "xsp": ("sbuf", [128, 384], "uint8"),
+    "xsq": ("sbuf", [128, 512], F8), "xsp": ("sbuf", [128, 512], "uint8"),
     "c1q": ("sbuf", [128, K], F8), "c1p": ("sbuf", [128, K], "uint8"),
     "c1sq": ("sbuf", [128, K], F8), "c1sp": ("sbuf", [128, K], "uint8"),
     "c2q": ("sbuf", [128, N * K], F8), "c2p": ("sbuf", [128, N * K], "uint8"),
     "eq": ("sbuf", [128, 512], F8), "ep": ("sbuf", [128, 512], "uint8"),
     "hq": ("sbuf", [128, 1024], F8), "hp": ("sbuf", [128, 1024], "uint8"),
-    "crq": ("sbuf", [128, 256], F8), "crp": ("sbuf", [128, 256], "uint8"),
+    "crq": ("sbuf", [128, 640], F8), "crp": ("sbuf", [128, 640], "uint8"),
     "cdq": ("sbuf", [128, 1024], F8), "cdp": ("sbuf", [128, 1024], "uint8"),
     "rq": ("sbuf", [128, 128], F8), "rp": ("sbuf", [128, 128], "uint8"),
-    "mw": ("sbuf", [128, 32], "int32"), "mw2": ("sbuf", [128, 32], "int32"), "mt": ("sbuf", [128, 32], "float32"),
-    "mask": ("sbuf", [128, 32], "float32"), "rst": ("sbuf", [128, 96], "float32"), "neg": ("sbuf", [128, 512], "bfloat16"),
-    "pi": ("sbuf", [128, 8], "int32"), "pidx": ("sbuf", [128, 8], "float32"), "pj": ("sbuf", [128, 8], "float32"),
-    "m": ("sbuf", [128, 3 * K], "float32"), "junk": ("sbuf", [128, 3 * K], "bfloat16"), "val": ("sbuf", [128, 16], "float32"),
+    "mw": ("sbuf", [128, 64], "int32"), "mw2": ("sbuf", [128, 64], "int32"), "mt": ("sbuf", [128, 32], "float32"),
+    "mask4": ("sbuf", [128, 32], "float32"), "mask16": ("sbuf", [128, 32], "float32"),
+    "rst4": ("sbuf", [128, 32], "float32"), "rst16": ("sbuf", [128, 96], "float32"), "neg": ("sbuf", [128, 512], "bfloat16"),
+    "pi": ("sbuf", [128, 8], "int32"), "pidx": ("sbuf", [128, 16], "float32"), "pj": ("sbuf", [128, 8], "float32"),
+    "m": ("sbuf", [128, 4 * K], "float32"), "junk": ("sbuf", [128, 4 * K], "bfloat16"), "val": ("sbuf", [128, 16], "float32"),
     "lb": ("sbuf", [128, 160], "float32"), "lt": ("sbuf", [128, 160], "float32"), "ls": ("sbuf", [128, 160], "float32"),
-    "lo": ("sbuf", [128, 160], "uint16"), "sbo": ("sbuf", [128, 16], "float32"),
-    "lst": ("sbuf", [128, 160], "uint16"), "sb": ("sbuf", [128, 32], "float32"),
-    "sel": ("sbuf", [128, 64], "float32"),
+    "lo": ("sbuf", [128, 64], "uint16"), "sbo": ("sbuf", [128, 16], "float32"),
+    "lst": ("sbuf", [128, 40], "uint16"), "sb": ("sbuf", [128, 32], "float32"),
+    "sel": ("sbuf", [128, 64], "float32"), "won": ("sbuf", [128, 4], "float32"),
     "dw1": ("sbuf", [128, 4 * 1024], "bfloat16"), "dw2": ("sbuf", [128, 4 * N * K], "bfloat16"),
     "m2": ("sbuf", [128, N * K], "float32"), "junk2": ("sbuf", [128, N * K], "bfloat16"),
-    "cnt": ("sbuf", [128, 32], "float32"), "yo": ("sbuf", [128, 512], "float32"),
+    "cnt": ("sbuf", [128, 64], "float32"), "yo": ("sbuf", [128, 512], "float32"),
     "ps": ("psum", [128, 4096], "float32"),
 }
 WID = [O["h0"], K - O["h0"]]
 for _h in range(2):
-    for _j in range(3):
+    for _j in range(4):
         SCRATCH["bq%d%d" % (_h, _j)] = ("dram" if O["dram"] else "sbuf", [128, WID[_h]], F8)
         SCRATCH["bp%d%d" % (_h, _j)] = ("dram" if O["dram"] else "sbuf", [128, WID[_h]], "uint8")
-SEMAPHORES = (["cv", "cs", "ct", "cg", "dx", "dc1", "dc2", "dout", "lsem", "xr", "xrp", "c1s", "c1sp", "c2b", "c2bp", "sbs"]
-              + ["xs%d" % i for i in range(3)] + ["cr%d" % i for i in range(2)] + ["crp%d" % i for i in range(2)]
+SEMAPHORES = (["cv", "cs", "ct", "cg", "dx", "dc1", "dc2", "dst", "dout", "lsem", "xr", "xrp", "c1s", "c1sp", "c2b", "c2bp", "sbs", "wl", "cl", "clp", "sbr"]
+              + ["xs%d" % i for i in range(4)] + ["cr%d" % i for i in range(2)] + ["crp%d" % i for i in range(2)]
               + ["mr%d" % i for i in range(4)] + ["mrp%d" % i for i in range(4)]
-              + ["l%d" % i for i in range(3)] + ["cd%d" % i for i in range(8)] + ["c2a%d" % i for i in range(8)])
+              + ["l%d" % i for i in range(2)] + ["cd%d" % i for i in range(8)] + ["c2a%d" % i for i in range(8)])
 MUL, ADD, MAX, MIN = AluOpType.mult, AluOpType.add, AluOpType.max, AluOpType.min
 COPY, SIGN = ActivationFunctionType.Copy, ActivationFunctionType.Sign
 
@@ -73,7 +77,7 @@ def rank_program(g, core, T, topo):
         ports = near([p for p in topo.cores_of(c) if topo.may_write(p, mate[0])])
         rest = near([p for p in topo.cores_of(c) if p != c and p not in ports])
         back = near([p for p in mate if topo.may_write(p, c)])
-        return ports[0::2], ports[1::2], rest[0:2], [back[0:2], back[2:4]]
+        return ports[0::2], ports[1::2], rest, [back[0:2], back[2:4]]
 
     def kx(a, b):
         return (pos(a) + pos(b)) % 4
@@ -82,29 +86,35 @@ def rank_program(g, core, T, topo):
         return (pos(a) - pos(b)) % 4
 
     def place(a, b):
-        return {3: 4, 1: 5, 2: 6, 0: 7}[delta(a, b)] if same(a, b) else kx(a, b)
+        return 4 + (delta(a, b) - 1) % 4 if same(a, b) else kx(a, b)
 
     def direct(a, b):
         return delta(a, b) in O["ld"] if same(a, b) else kx(a, b) in O["fd"]
 
-    def road(a, b):
-        return (direct(a, b) == (O["car"] == "rd"), delta(a, b) if same(a, b) else kx(a, b), same(a, b))
+    def road(a, b, order):
+        return order.index(name(a, b))
 
     def relayed(b):
-        return sorted([a for a in range(N) if a != b and not direct(a, b)], key=lambda a: (turn(a, b), same(a, b)))
+        return sorted([a for a in range(N) if a != b and not direct(a, b)], key=lambda a: road(a, b, O["arr"]))
 
-    def by_w(a, b):
-        return same(a, b) == direct(a, b) and (same(a, b) or kx(a, b) not in O["bx"])
+    def name(a, b):
+        return ("l%d" % delta(a, b)) if same(a, b) else ("u%d" % kx(a, b))
+
+    def relay(a, b):
+        i = int(name(a, b) in O["rel1"])
+        return i, [c for c in relayed(b) if int(name(c, b) in O["rel1"]) == i].index(a)
 
     def carried(a, w):
-        return sorted([b for b in range(N) if b != a and by_w(a, b) == w], key=lambda b: road(a, b))
+        return sorted([b for b in range(N) if b != a and name(a, b) in O[w]], key=lambda b: road(a, b, O[w]))
 
-    def turn(a, b):
-        return carried(a, by_w(a, b)).index(b)
+    def judge(a):
+        return roles(a)[O["arb"]][0]
 
     X = sorted([b for b in range(N) if not same(me, b)], key=lambda b: kx(me, b))
-    Y = {delta(b, me): b for b in range(N) if b != me and same(b, me)}
+    Y = {delta(b, me): b for b in range(N) if same(b, me)}
     S, B, W, M = roles(me)
+    J = judge(me)
+    W = W[:2]
 
     eng = {"v": g.vector, "s": g.scalar, "t": g.tensor, "g": g, "y": g.sync}
     cnt = {"v": 0, "s": 0, "t": 0, "g": 0}
@@ -148,9 +158,12 @@ def rank_program(g, core, T, topo):
     def c8(t, a, b):
         return t[:, a:b].bitcast(dt.uint8)
 
-    def send_tiles(dq, dp, items):
-        send(dq, [(e, c8(q, a, a + n), [(c, c8(oq, z, z + n)) for c, oq, op, z in ds], sq) for e, q, p, a, n, ds, sq, sp in items])
-        send(dp, [(e, p[:, a:a + n], [(c, op[:, z:z + n]) for c, oq, op, z in ds], sp) for e, q, p, a, n, ds, sq, sp in items])
+    def send_tiles(dq, dp, items, only=O["pf"]):
+        for what in only:
+            if what == "q":
+                send(dq, [(e, c8(q, a, a + n), [(c, c8(oq, z, z + n)) for c, oq, op, z in ds], sq) for e, q, p, a, n, ds, sq, sp in items])
+            else:
+                send(dp or dq, [(e, p[:, a:a + n], [(c, op[:, z:z + n]) for c, oq, op, z in ds], sp) for e, q, p, a, n, ds, sq, sp in items])
 
     def finish():
         need("g", [("c" + q, n) for q, n in cnt.items() if n] + [(s, n) for s, n in tot.items()])
@@ -169,44 +182,104 @@ def rank_program(g, core, T, topo):
         return T["bq%d%d" % (h, j)], T["bp%d%d" % (h, j)]
 
     def x_out(k, e):
-        return (e, T.xrq, T.xrp, 0, 128, [(roles(X[k])[0][k // 2], T.xsq, T.xsp, 128 * (k % 2))], "xs%d" % (k % 2), "xs%d" % (k % 2))
+        return (e, T.xrq, T.xrp, 0, 128, [(roles(X[k])[0][k // 2 * O["two"]], T.xsq, T.xsp, 128 * k)], "xs%d" % k, "xs%d" % k)
 
-    if core in B or core in W:
-        h = (B if core in B else W).index(core)
-        if O["fw4"] and core in B:
-            send_tiles([("xr", NO)], [("xrp", NO)], [x_out(2 * h + 1, off)])
+    def list_tools(r):
+        mask, rst, z = T["mask%d" % r], T["rst%d" % r], 32 * (r == 4)
+        f = slice(z, z + 32)
+        k = do("g", [], lambda e: e.iota(T.mw[:, f], [[0, 2], [-1, r], [0, 16 // r]], 128, 1))
+        kr = do("v", [], lambda e: e.memset(rst[:, :], 1.0))
+        kr = do("v", [kr], lambda e: e.memset(rst[:, 0:rst.shape[1]:r], 0.0))
+        k = do("v", [k], lambda e: e.tensor_scalar(T.mw2[:, f], T.mw[:, f], r - 1, None, AluOpType.bitwise_and))
+        k = do("v", [k], lambda e: e.tensor_scalar(mask[:, :], T.mw2[:, f], 0.0, -65536.0, AluOpType.not_equal, MUL))
+        if r == 4:
+            kb = do("g", [], lambda e: e.iota(T.mt[:, :], [[0, 8], [1, 4]], 0, 0, allow_small_or_imprecise_dtypes=True))
+            kb = do("v", [kb], lambda e: e.tensor_scalar(T.mt[:, :], T.mt[:, :], 0.25, None, MUL))
+            k = do("v", [k, kb], lambda e: e.tensor_tensor(mask[:, :], mask[:, :], T.mt[:, :], ADD))
+        return [k, kr]
+
+    def build_lists(r, mask, vals, deps, w, z, turned):
+        n, u = 32 * len(vals), 32 // r
+        end = z + 4 * u * len(vals)
+        for i, v in enumerate(vals):
+            t = do("v", deps[i], lambda e: e.tensor_scalar(T.lb[:, w + 32 * i:w + 32 * i + 32], mask[:, :], v, 0.0, ADD, MAX))
+        t = do("v", [t], lambda e: e.transpose(T.lt[:, w:w + n], T.lb[:, w:w + n]))
+        t = do("v", [t], lambda e: e.tensor_tensor_scan(T.ls[:, w:w + n], T["rst%d" % r][:, 0:n], T.lt[:, w:w + n], 0.0, MUL, ADD))
+        for a in range(4):
+            o = T.lo[0:32, z + a:end:4] if turned else T.lo[0:32, z + u * a:z + u * a + u]
+            k = do("v", [t], lambda e: e.tensor_scalar(o, T.ls[32 * a:32 * a + 32, w + r - 1:w + n:r], 4.0 if r == 4 else 1.0, None, MUL))
+        k = do("v", [k], lambda e: e.tensor_copy(T.lo[32:64, z:end], T.lo[0:32, z:end]))
+        return do("v", [k], lambda e: e.tensor_copy(T.lo[64:128, z:end], T.lo[0:64, z:end]))
+
+    if core == J:
+        k16 = list_tools(16)
+        k_p = do("g", [], lambda e: e.iota(T.pi[:, 0:1], [[0, 1]], 0, 1))
+        k_q = do("g", [], lambda e: e.iota(T.pidx[:, :], [[128, 16]], 0, 0, allow_small_or_imprecise_dtypes=True))
+        k = do("v", [k_p], lambda e: e.tensor_scalar(T.pi[:, 1:2], T.pi[:, 0:1], 96, None, AluOpType.bitwise_and))
+        k = do("v", [k_p], lambda e: e.tensor_scalar(T.pi[:, 2:3], T.pi[:, 0:1], 16, None, AluOpType.bitwise_and))
+        k = do("v", [k_p], lambda e: e.tensor_scalar(T.pi[:, 3:4], T.pi[:, 0:1], 15, None, AluOpType.bitwise_and))
+        k = do("v", [k], lambda e: e.tensor_copy(T.pj[:, 0:3], T.pi[:, 1:4]))
+        k = do("v", [k], lambda e: e.tensor_scalar(T.pj[:, 4:5], T.pj[:, 0:1], 0.5, T.pj[:, 2:3], MUL, ADD))
+        k = do("v", [k], lambda e: e.tensor_scalar(T.pj[:, 5:6], T.pj[:, 1:2], 4.0, T.pj[:, 4:5], MUL, ADD))
+        k_p = do("v", [k, k_q], lambda e: e.tensor_scalar(T.pidx[:, :], T.pidx[:, :], T.pj[:, 5:6], None, ADD))
+        k_z = do("v", [], lambda e: e.memset(T.sel[:, 0:4], 0.0))
+    group = {"S": S, "B": B, "W": W}
+
+    def carry(w):
+        h = group[w].index(core)
         q, p = slot(h, 0)
         dq, dp = [("c2b", O.get("nb", Q4))], [("c2bp", O.get("nb", Q4))]
-        for b in carried(me, core in W):
+        for b in carried(me, w):
             if direct(me, b):
                 send_tiles(dq, dp, [(off, q, p, 0, WID[h], [(cores[b], T.c2q, T.c2p, me * K + WID[0] * h)], "c2a%d" % me, "c2a%d" % me)])
             else:
-                i = relayed(b).index(me)
-                send_tiles(dq, dp, [(off, q, p, 0, WID[h], [(roles(b)[3][h][i % 2],) + slot(h, i // 2) + (0,)], "mr%d" % (i // 2), "mrp%d" % (i // 2))])
-        finish()
-        return
+                i, j = relay(me, b)
+                send_tiles(dq, dp, [(off, q, p, 0, WID[h], [(roles(b)[3][h][i],) + slot(h, j) + (0,)], "mr%d" % j, "mrp%d" % j)])
+
+    def back(b, e, q, p, z):
+        s = place(b, me)
+        return (e, q, p, z, 128, [(cores[b], T.cdq, T.cdp, 128 * s)], "cd%d" % s, "cd%d" % s)
+
+    helper = {d: group[O["help"][2 * d - 2]][int(O["help"][2 * d - 1])] for d in (1, 2, 3)}
+    lanes = {1: {3: high}, 2: {2: share(high, 2)[0], 3: share(high, 2)[1]}, 3: {1: off, 2: share(high, 2)[0], 3: share(high, 2)[1]}}[len(O["via"])]
+
+    def hand_on():
+        for d in O["via"]:
+            if helper[d] == core:
+                send_tiles([("cl", len(lanes[d]))], [("clp", len(lanes[d]))], [back(Y[d], off, T.crq, T.crp, 256)])
+
+    if O["fw4"] and core in B:
+        send_tiles([("xr", NO)], [("xrp", NO)], [x_out(2 + B.index(core), off)])
+    for w in "BW":
+        if core in group[w]:
+            carry(w)
+            hand_on()
+    if core == J:
+        sel = T.sel
+        sc, nu = T.sb[:, 0:32:4], T.sb[:, 1:32:4]
+        k = do("v", [k_z, ("sbs", (3 + O["cv"]) * NO)], lambda e: e.tensor_reduce(sel[:, 0:1], sc, AxisListType.X, MAX))
+        k = do("v", [k], lambda e: e.tensor_scalar(sel[:, 8:16], sc, sel[:, 0:1], 16384.0, AluOpType.is_lt, MUL))
+        k = do("v", [k], lambda e: e.tensor_tensor(sel[:, 16:24], sel[:, 8:16], nu, ADD))
+        k = do("v", [k], lambda e: e.tensor_reduce(sel[:, 1:2], sel[:, 16:24], AxisListType.X, MIN))
+        k = do("v", [k], lambda e: e.tensor_scalar(sel[:, 24:32], nu, sel[:, 1:2], None, AluOpType.is_equal))
+        k = do("v", [k, k_p], lambda e: e.tensor_tensor(sel[:, 32:40], sel[:, 24:32], T.pidx[:, 0:8], MUL))
+        k = do("v", [k], lambda e: e.tensor_reduce(sel[:, 4:5], sel[:, 32:40], AxisListType.X, ADD))
+        k = build_lists(16, T.mask16, [sel[:, 4:5]], [[k] + k16], 0, 0, False)
+        e = share(high if O["je"] == "high" else off, 2)
+        send([k], [(e[0], T.lo[:, 0:8], [(rc, T.lst[:, 32:40])], "wl"), (e[1], sel[:, 0:4], [(rc, T.won[:, :])], "wl")])
     if core in M[0] + M[1]:
         h = int(core in M[1])
-        for i, a in enumerate(relayed(me)):
-            if M[h][i % 2] == core:
-                j = i // 2
+        for a in relayed(me):
+            i, j = relay(a, me)
+            if M[h][i] == core:
                 q, p = slot(h, j)
                 send_tiles([("mr%d" % j, NO)], [("mrp%d" % j, NO)], [(off, q, p, 0, WID[h], [(rc, T.c2q, T.c2p, a * K + WID[0] * h)], "c2a%d" % a, "c2a%d" % a)])
+    if core != rc and core not in S:
         finish()
         return
-    if core != rc and core not in S:
-        return
 
-    k_a = do("g", [], lambda e: e.iota(T.mw[:, :], [[0, 2], [-1, 4], [0, 4]], 128, 1))
-    k_b = do("g", [], lambda e: e.iota(T.mt[:, :], [[0, 8], [1, 4]], 0, 0, allow_small_or_imprecise_dtypes=True))
+    k16 = list_tools(16)
     k_neg = do("v", [], lambda e: e.memset(T.neg[:, :], BIG))
-    k_r = do("v", [], lambda e: e.memset(T.rst[:, :], 1.0))
-    k_r = do("v", [k_r], lambda e: e.memset(T.rst[:, 0:96:4], 0.0))
-    k_m = do("v", [k_a], lambda e: e.tensor_scalar(T.mw2[:, :], T.mw[:, :], 3, None, AluOpType.bitwise_and))
-    k_m = do("v", [k_m], lambda e: e.tensor_scalar(T.lb[:, 0:32], T.mw2[:, :], 0.0, -65536.0, AluOpType.not_equal, MUL))
-    k_b = do("v", [k_b], lambda e: e.tensor_scalar(T.lt[:, 0:32], T.mt[:, :], 0.25, None, MUL))
-    k_m = do("v", [k_m, k_b], lambda e: e.tensor_tensor(T.mask[:, :], T.lb[:, 0:32], T.lt[:, 0:32], ADD))
-
     banks = {"n": 0, "free": [[] for _ in range(8)]}
 
     def product(deps, lq, lp, a, rq, rp, b, n):
@@ -216,18 +289,6 @@ def rank_program(g, core, T, topo):
         t = do("t", list(deps) + banks["free"][i], lambda e: e.matmul_mx(o, lq[:, a:a + 128], lp[:, a:a + 128], rq[:, b:b + n], rp[:, b:b + n], True, True))
         return i, t
 
-    def build_lists(vals, deps, z, turned, mask=T.mask):
-        n = 32 * len(vals)
-        for i, v in enumerate(vals):
-            t = do("v", list(deps[i]) + [k_m], lambda e: e.tensor_scalar(T.lb[:, z + 32 * i:z + 32 * i + 32], mask[:, :], v, 0.0, ADD, MAX))
-        t = do("v", [t], lambda e: e.transpose(T.lt[:, z:z + n], T.lb[:, z:z + n]))
-        t = do("v", [t, k_r], lambda e: e.tensor_tensor_scan(T.ls[:, z:z + n], T.rst[:, 0:n], T.lt[:, z:z + n], 0.0, MUL, ADD))
-        for a in range(4):
-            o = T.lo[0:32, z + a:z + n:4] if turned else T.lo[0:32, z + 8 * a:z + 8 * a + 8]
-            u = do("v", [t], lambda e: e.tensor_scalar(o, T.ls[32 * a:32 * a + 32, z + 3:z + n:4], 4.0, None, MUL))
-        u = do("v", [u], lambda e: e.tensor_copy(T.lo[32:64, z:z + n], T.lo[0:32, z:z + n]))
-        return do("v", [u], lambda e: e.tensor_copy(T.lo[64:128, z:z + n], T.lo[0:64, z:z + n]))
-
     def score(deps, xq, xp, a, cq, cp, i):
         b, t = product(deps, xq, xp, a, cq, cp, 0, K)
         m = T.m[:, K * i:K * i + K]
@@ -236,41 +297,53 @@ def rank_program(g, core, T, topo):
         tv = do("s", [ts], lambda e: e.activation(T.junk[:, K * i:K * i + K], m, SIGN, bias=T.m[:, K * i + K - 1:K * i + K], scale=-1.0, accum_out=T.val[:, 4 * i:4 * i + 1]))
         return ts, tv
 
-    def tell(i, st, dst, d):
-        do("s", [st[0]], lambda e: e.activation(dst[:, d:d + 1], T.m[:, K * i + K - 1:K * i + K], COPY))
-        return do("s", [st[1]], lambda e: e.activation(dst[:, d + 1:d + 2], T.val[:, 4 * i:4 * i + 1], COPY, bias=float(me * K)))
+    def tell(i, st):
+        do("s", [st[0]], lambda e: e.activation(T.sbo[:, 4 * i:4 * i + 1], T.m[:, K * i + K - 1:K * i + K], COPY))
+        return do("s", [st[1]], lambda e: e.activation(T.sbo[:, 4 * i + 1:4 * i + 2], T.val[:, 4 * i:4 * i + 1], COPY, bias=float(me * K)))
 
     def claim(b, i, e):
         p = 4 * place(b, me)
-        return (e, T.sbo[:, 4 * i:4 * i + 2], [(cores[b], T.sb[:, p:p + 2])], "sbs")
+        return (e, T.sbo[:, 4 * i:4 * i + 2], [(judge(b), T.sb[:, p:p + 2])], "sbs")
 
     val = lambda i: T.val[:, 4 * i:4 * i + 1]
 
     if core in S:
         s = S.index(core)
-        owners = [X[2 * s], X[2 * s + 1]]
         if O["fw4"]:
-            send_tiles([("xr", NO)], [("xrp", NO)], [x_out(2 * s, off)])
+            send_tiles([("xr", NO)], [("xrp", NO)], [x_out(s, off)])
+        elif O["sq"]:
+            for i in range(2):
+                send_tiles([("xr", NO)], [("xrp", NO)], [x_out(2 * i + s, off)])
         else:
             send_tiles([("xr", NO)], [("xrp", NO)], [x_out(2 * s + i, halves[i]) for i in range(2)])
-        if O["fwd"] and s == 0:
-            send_tiles([("c1s", NO)], [("c1sp", NO)], [(high, T.c1sq, T.c1sp, 0, K, [(S[1], T.c1sq, T.c1sp, 0)], "c1s", "c1sp")])
-        c1 = [("c1s", NO), ("c1sp", NO)]
-        st = [score(c1 + [("xs%d" % i, NO * (1 + O["fw4"]))], T.xsq, T.xsp, 128 * i, T.c1sq, T.c1sp, i) for i in range(2)]
-        tl = build_lists([val(0), val(1)], [[st[0][1]], [st[1][1]]], 0, True)
-        send([tl], [(off, T.lo[:, 0:64], [(rc, T.lst[:, 64 * s:64 * s + 64])], "l%d" % s)])
-        tb = [tell(i, st[i], T.sbo, 4 * i) for i in range(2)]
-        send(tb, [claim(owners[i], i, halves[i]) for i in range(2)])
-        if s == O.get("s3", 1):
-            s3 = score([("xs2", 2 * NO)], T.xsq, T.xsp, 256, T.c1sq, T.c1sp, 2)
-            tl = build_lists([val(2)], [[s3[1]]], 64, True)
-            send([tl], [(off, T.lo[:, 64:96], [(rc, T.lst[:, 128:160])], "l2")])
-            tb = tell(2, s3, T.sbo, 8)
-            send([tb], [claim(Y[3], 2, off)])
+        carry("S")
+        if O["two"]:
+            c1 = [("c1s", NO), ("c1sp", NO)]
+            st = [score(c1 + [("xs%d" % j, 2 * NO)], T.xsq, T.xsp, 128 * j, T.c1sq, T.c1sp, j) for j in (2 * s, 2 * s + 1)]
+            tl = build_lists(16, T.mask16, [val(2 * s), val(2 * s + 1)], [[st[0][1]] + k16, [st[1][1]]], 0, 0, True)
+            tb = [tell(2 * s + j, st[j]) for j in range(2)]
+            send([tl], [(off, T.lo[:, 0:16], [(rc, T.lst[:, 16 * s:16 * s + 16])], "l%d" % s)])
+            send(tb, [claim(X[j], j, halves[j % 2]) for j in (2 * s, 2 * s + 1)])
+        elif s == 0:
+            c1 = [("c1s", NO), ("c1sp", NO)]
+            st = []
+            for i in range(2):
+                while len(st) < O["ahead"][i]:
+                    j = len(st)
+                    st.append(score(c1 + [("xs%d" % j, NO * (1 + O["fw4"] + O["sq"]))], T.xsq, T.xsp, 128 * j, T.c1sq, T.c1sp, j))
+                if i == 1:
+                    tb = [tell(j, st[j]) for j in range(4)]
+                tl = build_lists(16, T.mask16, [val(2 * i), val(2 * i + 1)], [[st[2 * i][1]] + k16, [st[2 * i + 1][1]]], 64 * i, 16 * i, True)
+                send([tl], [(high if O["le"] == "high" else off, T.lo[:, 16 * i:16 * i + 16], [(rc, T.lst[:, 16 * i:16 * i + 16])], "l%d" % i)])
+            for i in range(2):
+                send(tb, [claim(X[j], j, halves[j % 2]) for j in (2 * i, 2 * i + 1)])
+        if s == 1 and O["cv"]:
+            for i in range(2):
+                send([("sbr", NO)], [claim(Y[j], j, halves[j % 2]) for j in (2 * i, 2 * i + 1)])
+        hand_on()
         for i in range(2):
-            b = X[2 * i + s]
-            p = place(b, me)
-            send_tiles([("cr%d" % i, NO)], [("crp%d" % i, NO)], [(off, T.crq, T.crp, 128 * i, 128, [(cores[b], T.cdq, T.cdp, 128 * p)], "cd%d" % p, "cd%d" % p)])
+            ne = NO if (2 * i, 2) in O["rounds"] else 2 * NO
+            send_tiles([("cr%d" % i, ne)], [("crp%d" % i, ne)], [back(X[2 * i + s], off, T.crq, T.crp, 128 * i)])
         finish()
         return
 
@@ -281,55 +354,61 @@ def rank_program(g, core, T, topo):
         else:
             l_2 = load("y", "dc2", T.c2b[:, :], T.c2[:, :])
     k_w = do("g", [], lambda e: e.iota(T.ew[:, :], [[1, 528]], -3, -4, allow_small_or_imprecise_dtypes=True))
-    k_p = do("g", [], lambda e: e.iota(T.pi[:, 0:1], [[0, 1]], 0, 1))
-    k_q = do("g", [], lambda e: e.iota(T.pidx[:, :], [[128, 8]], 0, 0, allow_small_or_imprecise_dtypes=True))
+    k4 = list_tools(4)
+    k_o = do("g", [], lambda e: e.iota(T.pidx[:, :], [[O["run"], 16]], 0, 0, allow_small_or_imprecise_dtypes=True))
     k_d = do("v", [k_w], lambda e: e.tensor_scalar(T.eb[:, :], T.ew[:, :], 0.0, None, AluOpType.is_equal))
     q_x = do("v", [l_x], lambda e: e.quantize_mx(T.xq[:, :], T.xp[:, :], T.xb[:, :]))
     for t in range(4):
         k_e = do("v", [k_d], lambda e: e.quantize_mx(T.eq[:, 128 * t:128 * t + 128], T.ep[:, 128 * t:128 * t + 128], T.eb[:, 3 - t:515 - t]))
     like = {delta(me, b): b for b in Y.values()}
-    xo = [(cores[like[1]], T.xsq, T.xsp, 0), (cores[like[2]], T.xsq, T.xsp, 128), (roles(like[3])[0][O.get("s3", 1)], T.xsq, T.xsp, 256)]
     o2 = me * K
     for b in O["load"]:
         if b == "1":
             q_1 = do("v", [l_1], lambda e: e.quantize_mx(T.c1q[:, :], T.c1p[:, :], T.c1b[:, :]))
         else:
             q_2 = do("v", [l_2], lambda e: e.quantize_mx(T.c2q[:, o2:o2 + K], T.c2p[:, o2:o2 + K], T.c2b[:, :]))
+    if O["dram"] == 2:
+        for h in range(2):
+            q, p = slot(h, 0)
+            z = o2 + WID[0] * h
+            load("y", "dst", c8(q, 0, WID[h]), c8(T.c2q, z, z + WID[h]), [q_2])
+            staged = load("s", "dst", p[:, :], T.c2p[:, z:z + WID[h]], [q_2])
+    part = lambda h: (slot(h, 0) + (0,) if O["dram"] == 2 else (T.c2q, T.c2p, o2 + WID[0] * h)) + (WID[h],)
+    s_2 = staged if O["dram"] == 2 else q_2
     for step in O["plan"]:
         if step == "x":
-            send_tiles([q_x], [], [(e, T.xq, T.xp, 0, 128, [(c, T.xrq, T.xrp, 0) for c in cs], "xr", "xrp") for e, cs in [(high, S), (off, B)][:1 + O["fw4"]]])
+            send_tiles([q_x], [], [(high, T.xq, T.xp, 0, 128, [(c, T.xrq, T.xrp, 0) for c in S], "xr", "xrp")])
+        if step in "yz":
+            send_tiles([q_x], [], [(off if step == "y" else high, T.xq, T.xp, 0, 128, [(c, T.xrq, T.xrp, 0) for c in B], "xr", "xrp")])
         if step == "l":
-            send_tiles([q_x], [], [(off, T.xq, T.xp, 0, 128, xo[:2], "xs0", "xs0")])
+            to = [(cores[like[d]], T.xsq, T.xsp, 128 * d - 128) for d in (1, 2, 3)]
+            send_tiles([q_x], [], [(off, T.xq, T.xp, 0, 128, to, "xs0", "xs0")], "pq" if O["l1c"] else "p")
+            for d in () if O["l1c"] else (1, 2, 3):
+                send_tiles([q_x], [], [(off, T.xq, T.xp, 0, 128, to[d - 1:d], "xs%d" % d, "xs0")], "q")
         if step == "2":
             four = share(high, 2) + share(off, 2)
-            if WID[0] == WID[1]:
-                send_tiles([q_2], [], [(four[i], T.c2q, T.c2p, o2 + WID[0] * (i % 2), WID[0], [((B + W)[i],) + slot(i % 2, 0) + (0,)], "c2b", "c2bp") for i in range(4)])
-            else:
-                for h in (1, 0):
-                    send_tiles([q_2], [], [(e, T.c2q, T.c2p, o2 + WID[0] * h, WID[h], [(c,) + slot(h, 0) + (0,)], "c2b", "c2bp") for c, e in [(B[h], high), (W[h], off)]])
-        if step in "BW":
-            for h in (1, 0):
-                send_tiles([q_2], [], [(high if step == "B" else off, T.c2q, T.c2p, o2 + WID[0] * h, WID[h], [((B if step == "B" else W)[h],) + slot(h, 0) + (0,)], "c2b", "c2bp")])
+            send_tiles([s_2], [], [(four[i],) + part(i % 2) + ([(group[O["g2"][i // 2]][i % 2],) + slot(i % 2, 0) + (0,)], "c2b", "c2bp") for i in range(4)])
+        if step in "SBW":
+            e = share(high, 2)
+            send_tiles([s_2], [], [(e[h],) + part(h) + ([(group[step][h],) + slot(h, 0) + (0,)], "c2b", "c2bp") for h in (0, 1)])
         if step == "1":
-            if O["fwd"]:
-                send_tiles([q_1], [], [(off, T.c1q, T.c1p, 0, K, [(S[0], T.c1sq, T.c1sp, 0)], "c1s", "c1sp")])
-            else:
-                send_tiles([q_1], [], [(e, T.c1q, T.c1p, 0, K, [(c, T.c1sq, T.c1sp, 0)], "c1s", "c1sp") for c, e in zip(S, [off, high])])
-    send_tiles([], [], [(off, T.xq, T.xp, 0, 128, xo[2:], "xs2", "xs2")])
-    k = do("v", [k_p], lambda e: e.tensor_scalar(T.pi[:, 1:2], T.pi[:, 0:1], 5, None, AluOpType.arith_shift_right))
-    k = do("v", [k_p], lambda e: e.tensor_scalar(T.pi[:, 2:3], T.pi[:, 0:1], 28, None, AluOpType.bitwise_and))
-    k = do("v", [k_p], lambda e: e.tensor_scalar(T.pi[:, 3:4], T.pi[:, 0:1], 3, None, AluOpType.bitwise_and))
-    k = do("v", [k], lambda e: e.tensor_copy(T.pj[:, 0:3], T.pi[:, 1:4]))
-    k = do("v", [k], lambda e: e.tensor_scalar(T.pj[:, 4:5], T.pj[:, 0:1], T.pj[:, 1:2], 4.0, ADD, MUL))
-    k_p = do("v", [k, k_q], lambda e: e.tensor_scalar(T.pidx[:, :], T.pidx[:, :], T.pj[:, 4:5], T.pj[:, 2:3], ADD, ADD))
+            send_tiles([q_1], [], [(high, T.c1q, T.c1p, 0, K, [(c, T.c1sq, T.c1sp, 0) for c in S[:1 + O["two"]]], "c1s", "c1sp")])
+        if step in "aef":
+            send_tiles([q_1], [], [(off if step == "f" else high, T.c1q, T.c1p, 0, K, [(S[step != "a"], T.c1sq, T.c1sp, 0)], "c1s", "c1sp")])
+        if step == "o":
+            send_tiles([q_1], [], [(e, T.c1q, T.c1p, 0, K, [(c, T.c1sq, T.c1sp, 0)], "c1s", "c1sp") for c, e in zip(S, [high, off])])
+        if step in "sbw":
+            send_tiles([s_2], [], [(halves[h],) + part(h) + ([(group[step.upper()][h],) + slot(h, 0) + (0,)], "c2b", "c2bp") for h in (0, 1)])
+    for t in range(4):
+        k_1 = do("s", [l_1], lambda e: e.activation(T.c1d[:, K * t:K * t + K], T.c1b[:, t:4 * K:4], COPY))
 
     NK = N * K
     k_w1, k_w2 = [], []
 
     def decode(q, p, z, n, out, deps, done, by="svsv"):
-        for t in range(4):
+        for t in [t for t in range(4) if by[t] != "-"]:
             i, k = product(list(deps) + [k_e], T.eq, T.ep, 128 * t, q, p, z, n)
-            o = out[:, 4 * z + t:4 * (z + n):4]
+            o = out(t, z, n)
             src = T.ps[:, 512 * i:512 * i + n]
             if by[t] == "v":
                 r = do("v", [k], lambda e: e.tensor_scalar(o, src, -1.0, None, MUL))
@@ -338,98 +417,111 @@ def rank_program(g, core, T, topo):
             banks["free"][i] = [r]
             done.append(r)
 
+    def decode1(p, n, deps):
+        decode(T.cdq, T.cdp, 128 * p, 128 * n, lambda t, z, n: T.dw1[:, 1024 * t + z:1024 * t + z + n], deps, k_w1)
+
     def decode2(a, by="svsv"):
-        decode(T.c2q, T.c2p, a * K, K, T.dw2, [("c2a%d" % a, 4 * NO)], k_w2, by)
+        decode(T.c2q, T.c2p, a * K, K, lambda t, z, n: T.dw2[:, 4 * z + t:4 * (z + n):4], [("c2a%d" % a, 4 * NO)] if a != me else [q_2], k_w2, by)
 
-    def gather(lst, a, n, cut, deps, z):
-        kv = do("v", deps, lambda e: e.tensor_copy(T.h[:, z:z + 16 * cut], T.c1b[:, :].indirect(lst[:, a:a + cut])))
-        ks = do("s", deps, lambda e: e.activation(T.h[:, z + 16 * cut:z + 16 * n], T.c1b[:, :].indirect(lst[:, a + cut:a + n]), COPY))
-        return [kv, ks]
-
-    def back(b, e, z):
-        p = place(b, me)
-        return (e, T.hq, T.hp, z, 128, [(cores[b], T.cdq, T.cdp, 128 * p)], "cd%d" % p, "cd%d" % p)
+    def gather(lst, a, n, deps, z, by="vvss"):
+        ks = []
+        for t in range(4):
+            o, w = T.h[:, z + t:z + 512 * n:4], T.c1d[:, K * t:K * t + K].indirect(lst[:, a:a + 8 * n])
+            if by[t] == "v":
+                ks.append(do("v", deps + [k_1], lambda e: e.tensor_copy(o, w)))
+            else:
+                ks.append(do("s", deps + [k_1], lambda e: e.activation(o, w, COPY)))
+        return ks
 
     st = [score([q_x, q_1], T.xq, T.xp, 0, T.c1q, T.c1p, 0)]
-    tl = build_lists([val(0)], [[st[0][1]]], 64, True)
-    t_sb = tell(0, st[0], T.sb, 28)
-    ga = gather(T.lo, 64, 32, 12, [tl, l_1], 3584)
+    tl = build_lists(16, T.mask16, [val(0)], [[st[0][1]] + k16], 0, 0, True)
+    tb = [do("v", [], lambda e: e.memset(T.sbo[:, :], 0.0))]
+    need("s", tb)
+    tb.append(tell(0, st[0]))
+    ga = gather(T.lo, 0, 1, [tl], 3584)
     q_own = do("v", ga, lambda e: e.quantize_mx(T.cdq[:, 896:1024], T.cdp[:, 896:1024], T.h[:, 3584:4096]))
-    decode(T.c2q, T.c2p, me * K, K, T.dw2, [q_2], k_w2)
-    st += [score([("xs0", 4 * NO)], T.xsq, T.xsp, 128 * i, T.c1q, T.c1p, 1 + i) for i in range(2)]
-    tl = build_lists([val(1), val(2)], [[st[1][1]], [st[2][1]]], 0, True)
-    tb = [tell(1 + i, st[1 + i], T.sbo, 4 * i) for i in range(2)]
-    send(tb, [claim(Y[1 + i], i, halves[i]) for i in range(2)])
-    ga = gather(T.lo, 0, 64, O["cut"], [tl], 0)
-    q = do("v", ga, lambda e: e.quantize_mx(T.hq[:, 0:256], T.hp[:, 0:256], T.h[:, 0:1024]))
-    send_tiles([q], [], [back(Y[1 + i], halves[i], 128 * i) for i in range(2)])
+    decode2(me)
+    def claims():
+        if O["cv"]:
+            send(tb, [(high, T.sbo[:, :], [(S[1], T.sbo[:, :])], "sbr")])
+        else:
+            send(tb, [claim(Y[d], d, share(off, 4)[d]) for d in range(4)])
+
+    for ds in O["batch"]:
+        st += [score([("xs0", 6 * NO)] if O["l1c"] else [("xs0", 3 * NO), ("xs%d" % d, NO)], T.xsq, T.xsp, 128 * d - 128, T.c1q, T.c1p, d) for d in ds]
+        tl = build_lists(16, T.mask16, [val(d) for d in ds], [[st[d][1]] for d in ds], 32 * ds[0], 8 * ds[0], True)
+        tb += [tell(d, st[d]) for d in ds]
+        z, n = 128 * ds[0] - 128, 128 * len(ds)
+        ga = gather(T.lo, 8 * ds[0], len(ds), [tl], 4 * z)
+        if ds[-1] == 3:
+            claims()
+        q = do("v", ga, lambda e: e.quantize_mx(T.hq[:, z:z + n], T.hp[:, z:z + n], T.h[:, 4 * z:4 * (z + n)]))
+        for d in ds:
+            if d not in O["via"]:
+                send_tiles([q], [], [back(Y[d], off, T.hq, T.hp, 128 * d - 128)])
+        send_tiles([q], [], [(lanes[d], T.hq, T.hp, 128 * d - 128, 128, [(helper[d], T.crq, T.crp, 256)], "cl", "clp") for d in O["via"]])
 
     far = [a for a in range(N) if a != me]
-    parts = sorted(far, key=lambda a: turn(a, me) + (0 if direct(a, me) else O.get("pen", 1.5)))
+    parts = sorted(far, key=lambda a: road(a, me, O["arr"]))
     for a in parts[:O["early"]]:
         decode2(a)
-    for i in range(2):
-        z = 256 + 256 * i
-        ga = gather(T.lst, 64 * i, 64, O["cut"], [("l%d" % i, NO)], 4 * z)
-        q = do("v", ga, lambda e: e.quantize_mx(T.hq[:, z:z + 256], T.hp[:, z:z + 256], T.h[:, 4 * z:4 * z + 1024]))
-        send_tiles([q], [], [(e, T.hq, T.hp, z + 128 * j, 128, [(S[j], T.crq, T.crp, 128 * i)], "cr%d" % i, "crp%d" % i) for j, e in enumerate([off, high])])
-    ga = gather(T.lst, 128, 32, 12, [("l2", NO)], 3072)
-    q = do("v", ga, lambda e: e.quantize_mx(T.hq[:, 768:896], T.hp[:, 768:896], T.h[:, 3072:3584]))
-    send_tiles([q], [], [back(Y[3], off, 768)])
-
-    decode(T.cdq, T.cdp, 640, 384, T.dw1, [q_own, ("cd5", NO), ("cd6", NO)], k_w1)
-
-    sel = T.sel
-    sc, nu = T.sb[:, 0:32:4], T.sb[:, 1:32:4]
-    k = do("v", [t_sb, ("sbs", 4 * NO)], lambda e: e.tensor_reduce(sel[:, 0:1], sc, AxisListType.X, MAX))
-    k = do("v", [k], lambda e: e.tensor_scalar(sel[:, 8:16], sc, sel[:, 0:1], 16384.0, AluOpType.is_lt, MUL))
-    k = do("v", [k], lambda e: e.tensor_tensor(sel[:, 16:24], sel[:, 8:16], nu, ADD))
-    k_n = do("v", [k], lambda e: e.tensor_reduce(sel[:, 1:2], sel[:, 16:24], AxisListType.X, MIN))
-    k = do("v", [k_n], lambda e: e.tensor_scalar(sel[:, 24:32], nu, sel[:, 1:2], None, AluOpType.is_equal))
-    k = do("v", [k, k_p], lambda e: e.tensor_tensor(sel[:, 32:40], sel[:, 24:32], T.pidx[:, :], MUL))
-    k = do("v", [k], lambda e: e.tensor_reduce(sel[:, 2:3], sel[:, 32:40], AxisListType.X, ADD))
-    k_l1 = build_lists([sel[:, 2:3]], [[k]], 96, False)
-    load("y", "dout", T.no[0:1, :], sel[:, 1:2], [k_n])
-    load("y", "dout", T.no[2:3, :], sel[:, 0:1], [k_n])
+    near = [q_own, ("cd4", 2 * NO), ("cd5", 2 * NO), ("cd6", 2 * NO)]
+    for a, n in O["rounds"]:
+        z, i = 384 + 128 * a, a // 2
+        ga = gather(T.lst, 8 * a, n, [("l%d" % i, NO)], 4 * z)
+        q = do("v", ga, lambda e: e.quantize_mx(T.hq[:, z:z + 128 * n], T.hp[:, z:z + 128 * n], T.h[:, 4 * z:4 * z + 512 * n]))
+        send_tiles([q], [], [(e, T.hq, T.hp, z + 128 * j, 128, [(S[(a + j) % 2], T.crq, T.crp, 128 * i)], "cr%d" % i, "crp%d" % i) for j, e in enumerate(share(onchip, n))])
+    load("y", "dout", T.no[0:1, :], T.won[:, 1:2], [("wl", NO)])
+    load("y", "dout", T.no[2:3, :], T.won[:, 0:1])
 
     nl = len(parts) - O["late"]
-    nm = nl - O["mid"]
-    for a in parts[O["early"]:nm]:
-        decode2(a)
-    decode(T.cdq, T.cdp, 0, 256, T.dw1, [("cd0", 2 * NO), ("cd1", 2 * NO)], k_w1)
-    for a in parts[nm:nl]:
-        decode2(a)
-    for p in (4, 3, 2):
-        decode(T.cdq, T.cdp, 128 * p, 128, T.dw1, [("cd%d" % p, 2 * NO)], k_w1)
-    k = do("v", [k_l1] + k_w1, lambda e: e.tensor_tensor(T.rb[:, :], T.dw1[:, :].indirect(T.lo[:, 96:128]), T.xb[:, :], ADD))
+    rest = parts[O["early"]:nl]
+    for step in O["seq"]:
+        if step == "p":
+            decode2(rest.pop(0))
+        if step == "q":
+            decode2(parts[nl + 1], O["l0"])
+        if step == "r":
+            decode2(parts[nl], O["k0"])
+        if step == "n":
+            decode1(4, 4, near)
+        if step == "a":
+            decode1(0, 2, [("cd0", 2 * NO), ("cd1", 2 * NO)])
+        if step == "b":
+            decode1(2, 2, [("cd2", 2 * NO), ("cd3", 2 * NO)])
+        if step in "0123":
+            decode1(int(step), 1, [("cd" + step, 2 * NO)])
+    assert not rest
+    for t in range(4):
+        k = do("v", [("wl", NO)] + k_w1, lambda e: e.tensor_tensor(T.rb[:, t:512:4], T.dw1[:, 1024 * t:1024 * t + 1024].indirect(T.lst[:, 32:40]), T.xb[:, t:512:4], ADD))
     q_r = do("v", [k], lambda e: e.quantize_mx(T.rq[:, :], T.rp[:, :], T.rb[:, :]))
-    for a in parts[nl:nl + 1]:
-        decode2(a, "ssss")
+    decode2(parts[nl], O["k1"])
+    decode2(parts[nl + 1], O["l1"])
 
-    n2 = NK // 512
-    last = []
+    n = O["run"]
+    n2 = NK // n
+    n1 = n2 - 1
     cn = []
     for i in range(n2):
-        b, k = product([q_r] + [("c2a%d" % a, 4 * NO) for a in parts], T.rq, T.rp, 0, T.c2q, T.c2p, 512 * i, 512)
-        z = 512 * i
-        ini = BIG if i == 0 else T.m2[:, z - 1:z]
-        k = do("v", [k] + last, lambda e: e.tensor_tensor_scan(T.m2[:, z:z + 512], T.ps[:, 512 * b:512 * b + 512], T.neg[:, :], ini, MAX, MAX))
-        banks["free"][b] = [k]
-        last = [k]
-        cn.append(do("s", [k], lambda e: e.activation(T.junk2[:, z:z + 512], T.m2[:, z:z + 512], SIGN, bias=T.m2[:, z + 511:z + 512], scale=-1.0, accum_out=T.cnt[:, i:i + 1])))
-    load("y", "dout", T.no[3:4, :], T.m2[:, NK - 1:NK], last)
-    n1 = n2 - 1
-    k = do("v", last, lambda e: e.tensor_scalar(T.cnt[:, 8:8 + n1], T.m2[:, 511:NK - 1:512], T.m2[:, NK - 1:NK], 512.0, AluOpType.is_lt, MUL))
-    k = do("v", [k] + cn[:n1], lambda e: e.tensor_tensor(T.cnt[:, 16:16 + n1], T.cnt[:, 8:8 + n1], T.cnt[:, 0:n1], MAX))
-    k_c = do("v", [k], lambda e: e.tensor_reduce(T.cnt[:, 24:25], T.cnt[:, 16:16 + n1], AxisListType.X, ADD))
-    k = do("v", [k_c], lambda e: e.tensor_scalar(T.mt[:, :], T.mask[:, :], T.cnt[:, 24:25], None, ADD))
-    k_n = do("s", [k_c, cn[n1]], lambda e: e.activation(T.cnt[:, 28:29], T.cnt[:, n1:n2], ActivationFunctionType.Identity, bias=T.cnt[:, 24:25]))
-    load("y", "dout", T.no[1:2, :], T.cnt[:, 28:29], [k_n])
-    for a in parts[nl + 1:]:
-        decode2(a, "svss")
-    k = build_lists([T.cnt[:, n1:n2]], [[k, cn[n1]]], 128, False, T.mt)
+        z = n * i
+        b, k = product([q_r] + [("c2a%d" % a, 4 * NO) for a in parts], T.rq, T.rp, 0, T.c2q, T.c2p, z, n)
+        last = do("v", [k], lambda e: e.tensor_tensor_scan(T.m2[:, z:z + n], T.ps[:, 512 * b:512 * b + n], T.neg[:, 0:n], BIG, MAX, MAX))
+        banks["free"][b] = [last]
+        cn.append(do("s", [last], lambda e: e.activation(T.junk2[:, z:z + n], T.m2[:, z:z + n], SIGN, bias=T.m2[:, z + n - 1:z + n], scale=-1.0, accum_out=T.cnt[:, i:i + 1])))
+        if i == n1:
+            k = do("v", cn[:n1] + [k_o], lambda e: e.tensor_tensor(T.cnt[:, 16:16 + n1], T.cnt[:, 0:n1], T.pidx[:, 0:n1], ADD))
+    ends = T.m2[:, n - 1:NK:n]
+    k_m = do("v", [last], lambda e: e.tensor_reduce(T.cnt[:, 48:49], ends, AxisListType.X, MAX))
+    load("y", "dout", T.no[3:4, :], T.cnt[:, 48:49], [k_m])
+    k = do("v", [k_m], lambda e: e.tensor_scalar(T.cnt[:, 32:32 + n1], T.m2[:, n - 1:NK - 1:n], T.cnt[:, 48:49], 16384.0, AluOpType.is_lt, MUL))
+    k = do("v", [k], lambda e: e.tensor_tensor(T.cnt[:, 52:52 + n1], T.cnt[:, 32:32 + n1], T.cnt[:, 16:16 + n1], ADD))
+    k_c = do("v", [k], lambda e: e.tensor_reduce(T.cnt[:, 49:50], T.cnt[:, 52:52 + n1], AxisListType.X, MIN))
+    decode2(parts[nl + 1], O["l2"])
+    k = do("v", [k_c, cn[n1]], lambda e: e.tensor_scalar(T.cnt[:, 50:51], T.cnt[:, n1:n2], float(n * n1), T.cnt[:, 49:50], ADD, MIN))
+    load("y", "dout", T.no[1:2, :], T.cnt[:, 50:51], [k])
+    k = build_lists(4, T.mask4, [T.cnt[:, 50:51]], [[k] + k4], 128, 32, False)
     for i, q in enumerate("sy"):
         f = slice(256 * i, 256 * i + 256)
-        r = do("v", [k] + k_w2, lambda e: e.tensor_tensor(T.yo[:, f], T.dw2[:, :].indirect(T.lo[:, 128 + 16 * i:144 + 16 * i]), T.rb[:, f], ADD))
+        r = do("v", [k] + k_w2, lambda e: e.tensor_tensor(T.yo[:, f], T.dw2[:, :].indirect(T.lo[:, 32 + 16 * i:48 + 16 * i]), T.rb[:, f], ADD))
         load(q, "dout", T.y[:, f], T.yo[:, f], [r])
     finish()

from concourse.bass import DstId, RemoteDMATransfer
from concourse.mybir import dt, AluOpType, AxisListType, ActivationFunctionType

N = 8
K = 384
WORLD = 256
BIG = -1.0e29
F8 = "float8_e4m3fn_x4"
O = dict(load="21", plan="xl2ae", fwd=0, car="dr", late=2, early=1, ld=(1, 2), fd=(0,), bx=(1,), h0=192, fw4=0, dram=2, mid=0,
         likeearly=0, runs=(128, 384, 512, 512, 512, 512, 512), arb=2, pf="pq", ra=0, g2="BW", S="", B="u0 l1 l2 l3", W="u1 u2 u3", rel1="u1 u3",
         arr="u0 l1 l2 u1 u2 l3 u3", lk=0, le="off", seq="pppnpa23", l1="v---", l2="-sss", k1="ssss", k0="sv--", l0="v---", cv=0, batch=((1, 2, 3),), via=(1, 2, 3), ahead=(2, 4), sq=1, l1c=0, two=1, help="W0W1S1", rounds=((0, 2), (2, 1), (3, 1)), run=384, je="off")
SCRATCH = {
    "xb": ("sbuf", [128, 512], "bfloat16"), "c1b": ("sbuf", [128, 4 * K], "bfloat16"), "c2b": ("sbuf", [128, 4 * K], "bfloat16"),
    "c1d": ("sbuf", [128, 4 * K], "bfloat16"),
    "ew": ("sbuf", [128, 528], "bfloat16"), "eb": ("sbuf", [128, 528], "bfloat16"), "h": ("sbuf", [128, 8 * 512], "bfloat16"),
    "rb": ("sbuf", [128, 512], "bfloat16"),
    "xq": ("sbuf", [128, 128], F8), "xp": ("sbuf", [128, 128], "uint8"),
    "xrq": ("sbuf", [128, 128], F8), "xrp": ("sbuf", [128, 128], "uint8"),
    "xsq": ("sbuf", [128, 512], F8), "xsp": ("sbuf", [128, 512], "uint8"),
    "c1q": ("sbuf", [128, K], F8), "c1p": ("sbuf", [128, K], "uint8"),
    "c1sq": ("sbuf", [128, K], F8), "c1sp": ("sbuf", [128, K], "uint8"),
    "c2q": ("sbuf", [128, N * K], F8), "c2p": ("sbuf", [128, N * K], "uint8"),
    "eq": ("sbuf", [128, 512], F8), "ep": ("sbuf", [128, 512], "uint8"),
    "hq": ("sbuf", [128, 1024], F8), "hp": ("sbuf", [128, 1024], "uint8"),
    "crq": ("sbuf", [128, 640], F8), "crp": ("sbuf", [128, 640], "uint8"),
    "cdq": ("sbuf", [128, 1024], F8), "cdp": ("sbuf", [128, 1024], "uint8"),
    "rq": ("sbuf", [128, 128], F8), "rp": ("sbuf", [128, 128], "uint8"),
    "mw": ("sbuf", [128, 64], "int32"), "mw2": ("sbuf", [128, 64], "int32"), "mt": ("sbuf", [128, 32], "float32"),
    "mask4": ("sbuf", [128, 32], "float32"), "mask16": ("sbuf", [128, 32], "float32"),
    "rst4": ("sbuf", [128, 32], "float32"), "rst16": ("sbuf", [128, 96], "float32"), "neg": ("sbuf", [128, 512], "bfloat16"),
    "pi": ("sbuf", [128, 8], "int32"), "pidx": ("sbuf", [128, 16], "float32"), "pj": ("sbuf", [128, 8], "float32"),
    "m": ("sbuf", [128, 4 * K], "float32"), "junk": ("sbuf", [128, 4 * K], "bfloat16"), "val": ("sbuf", [128, 16], "float32"),
    "lb": ("sbuf", [128, 160], "float32"), "lt": ("sbuf", [128, 160], "float32"), "ls": ("sbuf", [128, 160], "float32"),
    "lo": ("sbuf", [128, 64], "uint16"), "sbo": ("sbuf", [128, 16], "float32"),
    "lst": ("sbuf", [128, 40], "uint16"), "sb": ("sbuf", [128, 32], "float32"),
    "sel": ("sbuf", [128, 64], "float32"), "won": ("sbuf", [128, 4], "float32"),
    "dw1": ("sbuf", [128, 4 * 1024], "bfloat16"), "dw2": ("sbuf", [128, 4 * N * K], "bfloat16"),
    "m2": ("sbuf", [128, N * K], "float32"), "junk2": ("sbuf", [128, N * K], "bfloat16"),
    "cnt": ("sbuf", [128, 64], "float32"), "yo": ("sbuf", [128, 512], "float32"),
    "ps": ("psum", [128, 4096], "float32"),
}
WID = [O["h0"], K - O["h0"]]
for _h in range(2):
    for _j in range(4):
        SCRATCH["bq%d%d" % (_h, _j)] = ("dram" if O["dram"] else "sbuf", [128, WID[_h]], F8)
        SCRATCH["bp%d%d" % (_h, _j)] = ("dram" if O["dram"] else "sbuf", [128, WID[_h]], "uint8")
SEMAPHORES = (["cv", "cs", "ct", "cg", "dx", "dc1", "dc2", "dst", "dout", "lsem", "xr", "xrp", "c1s", "c1sp", "c2b", "c2bp", "sbs", "wl", "cl", "clp", "sbr"]
              + ["xs%d" % i for i in range(4)] + ["cr%d" % i for i in range(2)] + ["crp%d" % i for i in range(2)]
              + ["mr%d" % i for i in range(4)] + ["mrp%d" % i for i in range(4)]
              + ["l%d" % i for i in range(2)] + ["cd%d" % i for i in range(8)] + ["c2a%d" % i for i in range(8)])
MUL, ADD, MAX, MIN = AluOpType.mult, AluOpType.add, AluOpType.max, AluOpType.min
COPY, SIGN = ActivationFunctionType.Copy, ActivationFunctionType.Sign


def bits(engines):
    return sum(1 << e for e in engines)


def rank_program(g, core, T, topo):
    cores = list(T.cores)
    home = [a for a in range(N) if cores[a] in topo.cores_of(core) or topo.mates(core, cores[a])]
    if not home:
        return
    me = home[0]
    rc = cores[me]

    def same(a, b):
        return a == b or topo.same_plane(cores[a], cores[b])

    def pos(a):
        return [b for b in range(N) if same(a, b)].index(a)

    def roles(a):
        c = cores[a]
        mate = [p for p in range(WORLD) if topo.mates(c, p)]
        near = lambda ps: sorted(ps, key=lambda p: topo.die(p) != topo.die(c))
        ports = near([p for p in topo.cores_of(c) if topo.may_write(p, mate[0])])
        rest = near([p for p in topo.cores_of(c) if p != c and p not in ports])
        back = near([p for p in mate if topo.may_write(p, c)])
        return ports[0::2], ports[1::2], rest, [back[0:2], back[2:4]]

    def kx(a, b):
        return (pos(a) + pos(b)) % 4

    def delta(a, b):
        return (pos(a) - pos(b)) % 4

    def place(a, b):
        return 4 + (delta(a, b) - 1) % 4 if same(a, b) else kx(a, b)

    def direct(a, b):
        return delta(a, b) in O["ld"] if same(a, b) else kx(a, b) in O["fd"]

    def road(a, b, order):
        return order.index(name(a, b))

    def relayed(b):
        return sorted([a for a in range(N) if a != b and not direct(a, b)], key=lambda a: road(a, b, O["arr"]))

    def name(a, b):
        return ("l%d" % delta(a, b)) if same(a, b) else ("u%d" % kx(a, b))

    def relay(a, b):
        i = int(name(a, b) in O["rel1"])
        return i, [c for c in relayed(b) if int(name(c, b) in O["rel1"]) == i].index(a)

    def carried(a, w):
        return sorted([b for b in range(N) if b != a and name(a, b) in O[w]], key=lambda b: road(a, b, O[w]))

    def judge(a):
        return roles(a)[O["arb"]][0]

    X = sorted([b for b in range(N) if not same(me, b)], key=lambda b: kx(me, b))
    Y = {delta(b, me): b for b in range(N) if same(b, me)}
    S, B, W, M = roles(me)
    J = judge(me)
    W = W[:2]

    eng = {"v": g.vector, "s": g.scalar, "t": g.tensor, "g": g, "y": g.sync}
    cnt = {"v": 0, "s": 0, "t": 0, "g": 0}
    seen = {}
    tot = {}

    def need(q, deps):
        best = {}
        for s, n in deps:
            best[s] = max(best.get(s, 0), n)
        for s in best:
            if seen.get((q, s), 0) < best[s]:
                eng[q].wait_ge(T.sem[s], best[s])
                seen[(q, s)] = best[s]

    def do(q, deps, fn):
        need(q, deps)
        i = fn(eng[q])
        cnt[q] += 1
        i.then_inc(T.sem["c" + q], 1)
        return ("c" + q, cnt[q])

    def load(q, sem, out, in_, deps=()):
        need(q, deps)
        eng[q].dma_start(out, in_).then_inc(T.sem[sem], 16)
        tot[sem] = tot.get(sem, 0) + 16
        return (sem, tot[sem])

    def send(deps, transfers):
        need("g", deps)
        out = []
        for engines, src, dsts, sem in transfers:
            ids = []
            for c, _ in dsts:
                rid, pid = topo.addr(c, core)
                ids.append(DstId(rid=rid, pnc=pid))
            out.append(RemoteDMATransfer(dst_ids=ids, dma_engine_mask=bits(engines), remote_sem=T.sem[sem], srcs=[src], dsts=[d for _, d in dsts]))
            tot["lsem"] = tot.get("lsem", 0) + len(engines)
        g.remote_dma_fused(out, local_sem=T.sem["lsem"])

    def c8(t, a, b):
        return t[:, a:b].bitcast(dt.uint8)

    def send_tiles(dq, dp, items, only=O["pf"]):
        for what in only:
            if what == "q":
                send(dq, [(e, c8(q, a, a + n), [(c, c8(oq, z, z + n)) for c, oq, op, z in ds], sq) for e, q, p, a, n, ds, sq, sp in items])
            else:
                send(dp or dq, [(e, p[:, a:a + n], [(c, op[:, z:z + n]) for c, oq, op, z in ds], sp) for e, q, p, a, n, ds, sq, sp in items])

    def finish():
        need("g", [("c" + q, n) for q, n in cnt.items() if n] + [(s, n) for s, n in tot.items()])

    def share(engines, n):
        w = len(engines) // n
        return [engines[w * i:w * i + w] for i in range(n)]

    off = topo.engines(core, cores[Y[1]] if core in topo.cores_of(rc) else roles(Y[1])[3][0][0])
    onchip = topo.engines(core, [c for c in topo.cores_of(core) if c != core][0])
    high = [e for e in onchip if e not in off]
    NO, Q4 = len(off), len(onchip) // 4
    halves = share(off, 2)

    def slot(h, j):
        return T["bq%d%d" % (h, j)], T["bp%d%d" % (h, j)]

    def x_out(k, e):
        return (e, T.xrq, T.xrp, 0, 128, [(roles(X[k])[0][k // 2 * O["two"]], T.xsq, T.xsp, 128 * k)], "xs%d" % k, "xs%d" % k)

    def list_tools(r):
        mask, rst, z = T["mask%d" % r], T["rst%d" % r], 32 * (r == 4)
        f = slice(z, z + 32)
        k = do("g", [], lambda e: e.iota(T.mw[:, f], [[0, 2], [-1, r], [0, 16 // r]], 128, 1))
        kr = do("v", [], lambda e: e.memset(rst[:, :], 1.0))
        kr = do("v", [kr], lambda e: e.memset(rst[:, 0:rst.shape[1]:r], 0.0))
        k = do("v", [k], lambda e: e.tensor_scalar(T.mw2[:, f], T.mw[:, f], r - 1, None, AluOpType.bitwise_and))
        k = do("v", [k], lambda e: e.tensor_scalar(mask[:, :], T.mw2[:, f], 0.0, -65536.0, AluOpType.not_equal, MUL))
        if r == 4:
            kb = do("g", [], lambda e: e.iota(T.mt[:, :], [[0, 8], [1, 4]], 0, 0, allow_small_or_imprecise_dtypes=True))
            kb = do("v", [kb], lambda e: e.tensor_scalar(T.mt[:, :], T.mt[:, :], 0.25, None, MUL))
            k = do("v", [k, kb], lambda e: e.tensor_tensor(mask[:, :], mask[:, :], T.mt[:, :], ADD))
        return [k, kr]

    def build_lists(r, mask, vals, deps, w, z, turned):
        n, u = 32 * len(vals), 32 // r
        end = z + 4 * u * len(vals)
        for i, v in enumerate(vals):
            t = do("v", deps[i], lambda e: e.tensor_scalar(T.lb[:, w + 32 * i:w + 32 * i + 32], mask[:, :], v, 0.0, ADD, MAX))
        t = do("v", [t], lambda e: e.transpose(T.lt[:, w:w + n], T.lb[:, w:w + n]))
        t = do("v", [t], lambda e: e.tensor_tensor_scan(T.ls[:, w:w + n], T["rst%d" % r][:, 0:n], T.lt[:, w:w + n], 0.0, MUL, ADD))
        for a in range(4):
            o = T.lo[0:32, z + a:end:4] if turned else T.lo[0:32, z + u * a:z + u * a + u]
            k = do("v", [t], lambda e: e.tensor_scalar(o, T.ls[32 * a:32 * a + 32, w + r - 1:w + n:r], 4.0 if r == 4 else 1.0, None, MUL))
        k = do("v", [k], lambda e: e.tensor_copy(T.lo[32:64, z:end], T.lo[0:32, z:end]))
        return do("v", [k], lambda e: e.tensor_copy(T.lo[64:128, z:end], T.lo[0:64, z:end]))

    if core == J:
        k16 = list_tools(16)
        k_p = do("g", [], lambda e: e.iota(T.pi[:, 0:1], [[0, 1]], 0, 1))
        k_q = do("g", [], lambda e: e.iota(T.pidx[:, :], [[128, 16]], 0, 0, allow_small_or_imprecise_dtypes=True))
        k = do("v", [k_p], lambda e: e.tensor_scalar(T.pi[:, 1:2], T.pi[:, 0:1], 96, None, AluOpType.bitwise_and))
        k = do("v", [k_p], lambda e: e.tensor_scalar(T.pi[:, 2:3], T.pi[:, 0:1], 16, None, AluOpType.bitwise_and))
        k = do("v", [k_p], lambda e: e.tensor_scalar(T.pi[:, 3:4], T.pi[:, 0:1], 15, None, AluOpType.bitwise_and))
        k = do("v", [k], lambda e: e.tensor_copy(T.pj[:, 0:3], T.pi[:, 1:4]))
        k = do("v", [k], lambda e: e.tensor_scalar(T.pj[:, 4:5], T.pj[:, 0:1], 0.5, T.pj[:, 2:3], MUL, ADD))
        k = do("v", [k], lambda e: e.tensor_scalar(T.pj[:, 5:6], T.pj[:, 1:2], 4.0, T.pj[:, 4:5], MUL, ADD))
        k_p = do("v", [k, k_q], lambda e: e.tensor_scalar(T.pidx[:, :], T.pidx[:, :], T.pj[:, 5:6], None, ADD))
        k_z = do("v", [], lambda e: e.memset(T.sel[:, 0:4], 0.0))
    group = {"S": S, "B": B, "W": W}

    def carry(w):
        h = group[w].index(core)
        q, p = slot(h, 0)
        dq, dp = [("c2b", O.get("nb", Q4))], [("c2bp", O.get("nb", Q4))]
        for b in carried(me, w):
            if direct(me, b):
                send_tiles(dq, dp, [(off, q, p, 0, WID[h], [(cores[b], T.c2q, T.c2p, me * K + WID[0] * h)], "c2a%d" % me, "c2a%d" % me)])
            else:
                i, j = relay(me, b)
                send_tiles(dq, dp, [(off, q, p, 0, WID[h], [(roles(b)[3][h][i],) + slot(h, j) + (0,)], "mr%d" % j, "mrp%d" % j)])

    def back(b, e, q, p, z):
        s = place(b, me)
        return (e, q, p, z, 128, [(cores[b], T.cdq, T.cdp, 128 * s)], "cd%d" % s, "cd%d" % s)

    helper = {d: group[O["help"][2 * d - 2]][int(O["help"][2 * d - 1])] for d in (1, 2, 3)}
    lanes = {1: {3: high}, 2: {2: share(high, 2)[0], 3: share(high, 2)[1]}, 3: {1: off, 2: share(high, 2)[0], 3: share(high, 2)[1]}}[len(O["via"])]

    def hand_on():
        for d in O["via"]:
            if helper[d] == core:
                send_tiles([("cl", len(lanes[d]))], [("clp", len(lanes[d]))], [back(Y[d], off, T.crq, T.crp, 256)])

    if O["fw4"] and core in B:
        send_tiles([("xr", NO)], [("xrp", NO)], [x_out(2 + B.index(core), off)])
    for w in "BW":
        if core in group[w]:
            carry(w)
            hand_on()
    if core == J:
        sel = T.sel
        sc, nu = T.sb[:, 0:32:4], T.sb[:, 1:32:4]
        k = do("v", [k_z, ("sbs", (3 + O["cv"]) * NO)], lambda e: e.tensor_reduce(sel[:, 0:1], sc, AxisListType.X, MAX))
        k = do("v", [k], lambda e: e.tensor_scalar(sel[:, 8:16], sc, sel[:, 0:1], 16384.0, AluOpType.is_lt, MUL))
        k = do("v", [k], lambda e: e.tensor_tensor(sel[:, 16:24], sel[:, 8:16], nu, ADD))
        k = do("v", [k], lambda e: e.tensor_reduce(sel[:, 1:2], sel[:, 16:24], AxisListType.X, MIN))
        k = do("v", [k], lambda e: e.tensor_scalar(sel[:, 24:32], nu, sel[:, 1:2], None, AluOpType.is_equal))
        k = do("v", [k, k_p], lambda e: e.tensor_tensor(sel[:, 32:40], sel[:, 24:32], T.pidx[:, 0:8], MUL))
        k = do("v", [k], lambda e: e.tensor_reduce(sel[:, 4:5], sel[:, 32:40], AxisListType.X, ADD))
        k = build_lists(16, T.mask16, [sel[:, 4:5]], [[k] + k16], 0, 0, False)
        e = share(high if O["je"] == "high" else off, 2)
        send([k], [(e[0], T.lo[:, 0:8], [(rc, T.lst[:, 32:40])], "wl"), (e[1], sel[:, 0:4], [(rc, T.won[:, :])], "wl")])
    if core in M[0] + M[1]:
        h = int(core in M[1])
        for a in relayed(me):
            i, j = relay(a, me)
            if M[h][i] == core:
                q, p = slot(h, j)
                send_tiles([("mr%d" % j, NO)], [("mrp%d" % j, NO)], [(off, q, p, 0, WID[h], [(rc, T.c2q, T.c2p, a * K + WID[0] * h)], "c2a%d" % a, "c2a%d" % a)])
    if core != rc and core not in S:
        finish()
        return

    k16 = list_tools(16)
    k_neg = do("v", [], lambda e: e.memset(T.neg[:, :], BIG))
    banks = {"n": 0, "free": [[] for _ in range(8)]}

    def product(deps, lq, lp, a, rq, rp, b, n):
        i = banks["n"] % 8
        banks["n"] += 1
        o = T.ps[:, 512 * i:512 * i + n]
        t = do("t", list(deps) + banks["free"][i], lambda e: e.matmul_mx(o, lq[:, a:a + 128], lp[:, a:a + 128], rq[:, b:b + n], rp[:, b:b + n], True, True))
        return i, t

    def score(deps, xq, xp, a, cq, cp, i):
        b, t = product(deps, xq, xp, a, cq, cp, 0, K)
        m = T.m[:, K * i:K * i + K]
        ts = do("v", [t, k_neg], lambda e: e.tensor_tensor_scan(m, T.ps[:, 512 * b:512 * b + K], T.neg[:, 0:K], BIG, MAX, MAX))
        banks["free"][b] = [ts]
        tv = do("s", [ts], lambda e: e.activation(T.junk[:, K * i:K * i + K], m, SIGN, bias=T.m[:, K * i + K - 1:K * i + K], scale=-1.0, accum_out=T.val[:, 4 * i:4 * i + 1]))
        return ts, tv

    def tell(i, st):
        do("s", [st[0]], lambda e: e.activation(T.sbo[:, 4 * i:4 * i + 1], T.m[:, K * i + K - 1:K * i + K], COPY))
        return do("s", [st[1]], lambda e: e.activation(T.sbo[:, 4 * i + 1:4 * i + 2], T.val[:, 4 * i:4 * i + 1], COPY, bias=float(me * K)))

    def claim(b, i, e):
        p = 4 * place(b, me)
        return (e, T.sbo[:, 4 * i:4 * i + 2], [(judge(b), T.sb[:, p:p + 2])], "sbs")

    val = lambda i: T.val[:, 4 * i:4 * i + 1]

    if core in S:
        s = S.index(core)
        if O["fw4"]:
            send_tiles([("xr", NO)], [("xrp", NO)], [x_out(s, off)])
        elif O["sq"]:
            for i in range(2):
                send_tiles([("xr", NO)], [("xrp", NO)], [x_out(2 * i + s, off)])
        else:
            send_tiles([("xr", NO)], [("xrp", NO)], [x_out(2 * s + i, halves[i]) for i in range(2)])
        carry("S")
        if O["two"]:
            c1 = [("c1s", NO), ("c1sp", NO)]
            st = [score(c1 + [("xs%d" % j, 2 * NO)], T.xsq, T.xsp, 128 * j, T.c1sq, T.c1sp, j) for j in (2 * s, 2 * s + 1)]
            tl = build_lists(16, T.mask16, [val(2 * s), val(2 * s + 1)], [[st[0][1]] + k16, [st[1][1]]], 0, 0, True)
            tb = [tell(2 * s + j, st[j]) for j in range(2)]
            send([tl], [(off, T.lo[:, 0:16], [(rc, T.lst[:, 16 * s:16 * s + 16])], "l%d" % s)])
            send(tb, [claim(X[j], j, halves[j % 2]) for j in (2 * s, 2 * s + 1)])
        elif s == 0:
            c1 = [("c1s", NO), ("c1sp", NO)]
            st = []
            for i in range(2):
                while len(st) < O["ahead"][i]:
                    j = len(st)
                    st.append(score(c1 + [("xs%d" % j, NO * (1 + O["fw4"] + O["sq"]))], T.xsq, T.xsp, 128 * j, T.c1sq, T.c1sp, j))
                if i == 1:
                    tb = [tell(j, st[j]) for j in range(4)]
                tl = build_lists(16, T.mask16, [val(2 * i), val(2 * i + 1)], [[st[2 * i][1]] + k16, [st[2 * i + 1][1]]], 64 * i, 16 * i, True)
                send([tl], [(high if O["le"] == "high" else off, T.lo[:, 16 * i:16 * i + 16], [(rc, T.lst[:, 16 * i:16 * i + 16])], "l%d" % i)])
            for i in range(2):
                send(tb, [claim(X[j], j, halves[j % 2]) for j in (2 * i, 2 * i + 1)])
        if s == 1 and O["cv"]:
            for i in range(2):
                send([("sbr", NO)], [claim(Y[j], j, halves[j % 2]) for j in (2 * i, 2 * i + 1)])
        hand_on()
        for i in range(2):
            ne = NO if (2 * i, 2) in O["rounds"] else 2 * NO
            send_tiles([("cr%d" % i, ne)], [("crp%d" % i, ne)], [back(X[2 * i + s], off, T.crq, T.crp, 128 * i)])
        finish()
        return

    l_x = load("y", "dx", T.xb[:, :], T.x[:, :])
    for b in O["load"]:
        if b == "1":
            l_1 = load("y", "dc1", T.c1b[:, :], T.c1[:, :])
        else:
            l_2 = load("y", "dc2", T.c2b[:, :], T.c2[:, :])
    k_w = do("g", [], lambda e: e.iota(T.ew[:, :], [[1, 528]], -3, -4, allow_small_or_imprecise_dtypes=True))
    k4 = list_tools(4)
    k_o = do("g", [], lambda e: e.iota(T.pidx[:, :], [[O["run"], 16]], 0, 0, allow_small_or_imprecise_dtypes=True))
    k_d = do("v", [k_w], lambda e: e.tensor_scalar(T.eb[:, :], T.ew[:, :], 0.0, None, AluOpType.is_equal))
    q_x = do("v", [l_x], lambda e: e.quantize_mx(T.xq[:, :], T.xp[:, :], T.xb[:, :]))
    for t in range(4):
        k_e = do("v", [k_d], lambda e: e.quantize_mx(T.eq[:, 128 * t:128 * t + 128], T.ep[:, 128 * t:128 * t + 128], T.eb[:, 3 - t:515 - t]))
    like = {delta(me, b): b for b in Y.values()}
    o2 = me * K
    for b in O["load"]:
        if b == "1":
            q_1 = do("v", [l_1], lambda e: e.quantize_mx(T.c1q[:, :], T.c1p[:, :], T.c1b[:, :]))
        else:
            q_2 = do("v", [l_2], lambda e: e.quantize_mx(T.c2q[:, o2:o2 + K], T.c2p[:, o2:o2 + K], T.c2b[:, :]))
    if O["dram"] == 2:
        for h in range(2):
            q, p = slot(h, 0)
            z = o2 + WID[0] * h
            load("y", "dst", c8(q, 0, WID[h]), c8(T.c2q, z, z + WID[h]), [q_2])
            staged = load("s", "dst", p[:, :], T.c2p[:, z:z + WID[h]], [q_2])
    part = lambda h: (slot(h, 0) + (0,) if O["dram"] == 2 else (T.c2q, T.c2p, o2 + WID[0] * h)) + (WID[h],)
    s_2 = staged if O["dram"] == 2 else q_2
    for step in O["plan"]:
        if step == "x":
            send_tiles([q_x], [], [(high, T.xq, T.xp, 0, 128, [(c, T.xrq, T.xrp, 0) for c in S], "xr", "xrp")])
        if step in "yz":
            send_tiles([q_x], [], [(off if step == "y" else high, T.xq, T.xp, 0, 128, [(c, T.xrq, T.xrp, 0) for c in B], "xr", "xrp")])
        if step == "l":
            to = [(cores[like[d]], T.xsq, T.xsp, 128 * d - 128) for d in (1, 2, 3)]
            send_tiles([q_x], [], [(off, T.xq, T.xp, 0, 128, to, "xs0", "xs0")], "pq" if O["l1c"] else "p")
            for d in () if O["l1c"] else (1, 2, 3):
                send_tiles([q_x], [], [(off, T.xq, T.xp, 0, 128, to[d - 1:d], "xs%d" % d, "xs0")], "q")
        if step == "2":
            four = share(high, 2) + share(off, 2)
            send_tiles([s_2], [], [(four[i],) + part(i % 2) + ([(group[O["g2"][i // 2]][i % 2],) + slot(i % 2, 0) + (0,)], "c2b", "c2bp") for i in range(4)])
        if step in "SBW":
            e = share(high, 2)
            send_tiles([s_2], [], [(e[h],) + part(h) + ([(group[step][h],) + slot(h, 0) + (0,)], "c2b", "c2bp") for h in (0, 1)])
        if step == "1":
            send_tiles([q_1], [], [(high, T.c1q, T.c1p, 0, K, [(c, T.c1sq, T.c1sp, 0) for c in S[:1 + O["two"]]], "c1s", "c1sp")])
        if step in "aef":
            send_tiles([q_1], [], [(off if step == "f" else high, T.c1q, T.c1p, 0, K, [(S[step != "a"], T.c1sq, T.c1sp, 0)], "c1s", "c1sp")])
        if step == "o":
            send_tiles([q_1], [], [(e, T.c1q, T.c1p, 0, K, [(c, T.c1sq, T.c1sp, 0)], "c1s", "c1sp") for c, e in zip(S, [high, off])])
        if step in "sbw":
            send_tiles([s_2], [], [(halves[h],) + part(h) + ([(group[step.upper()][h],) + slot(h, 0) + (0,)], "c2b", "c2bp") for h in (0, 1)])
    for t in range(4):
        k_1 = do("s", [l_1], lambda e: e.activation(T.c1d[:, K * t:K * t + K], T.c1b[:, t:4 * K:4], COPY))

    NK = N * K
    k_w1, k_w2 = [], []

    def decode(q, p, z, n, out, deps, done, by="svsv"):
        for t in [t for t in range(4) if by[t] != "-"]:
            i, k = product(list(deps) + [k_e], T.eq, T.ep, 128 * t, q, p, z, n)
            o = out(t, z, n)
            src = T.ps[:, 512 * i:512 * i + n]
            if by[t] == "v":
                r = do("v", [k], lambda e: e.tensor_scalar(o, src, -1.0, None, MUL))
            else:
                r = do("s", [k], lambda e: e.activation(o, src, COPY, scale=-1.0))
            banks["free"][i] = [r]
            done.append(r)

    def decode1(p, n, deps):
        decode(T.cdq, T.cdp, 128 * p, 128 * n, lambda t, z, n: T.dw1[:, 1024 * t + z:1024 * t + z + n], deps, k_w1)

    def decode2(a, by="svsv"):
        decode(T.c2q, T.c2p, a * K, K, lambda t, z, n: T.dw2[:, 4 * z + t:4 * (z + n):4], [("c2a%d" % a, 4 * NO)] if a != me else [q_2], k_w2, by)

    def gather(lst, a, n, deps, z, by="vvss"):
        ks = []
        for t in range(4):
            o, w = T.h[:, z + t:z + 512 * n:4], T.c1d[:, K * t:K * t + K].indirect(lst[:, a:a + 8 * n])
            if by[t] == "v":
                ks.append(do("v", deps + [k_1], lambda e: e.tensor_copy(o, w)))
            else:
                ks.append(do("s", deps + [k_1], lambda e: e.activation(o, w, COPY)))
        return ks

    st = [score([q_x, q_1], T.xq, T.xp, 0, T.c1q, T.c1p, 0)]
    tl = build_lists(16, T.mask16, [val(0)], [[st[0][1]] + k16], 0, 0, True)
    tb = [do("v", [], lambda e: e.memset(T.sbo[:, :], 0.0))]
    need("s", tb)
    tb.append(tell(0, st[0]))
    ga = gather(T.lo, 0, 1, [tl], 3584)
    q_own = do("v", ga, lambda e: e.quantize_mx(T.cdq[:, 896:1024], T.cdp[:, 896:1024], T.h[:, 3584:4096]))
    decode2(me)
    def claims():
        if O["cv"]:
            send(tb, [(high, T.sbo[:, :], [(S[1], T.sbo[:, :])], "sbr")])
        else:
            send(tb, [claim(Y[d], d, share(off, 4)[d]) for d in range(4)])

    for ds in O["batch"]:
        st += [score([("xs0", 6 * NO)] if O["l1c"] else [("xs0", 3 * NO), ("xs%d" % d, NO)], T.xsq, T.xsp, 128 * d - 128, T.c1q, T.c1p, d) for d in ds]
        tl = build_lists(16, T.mask16, [val(d) for d in ds], [[st[d][1]] for d in ds], 32 * ds[0], 8 * ds[0], True)
        tb += [tell(d, st[d]) for d in ds]
        z, n = 128 * ds[0] - 128, 128 * len(ds)
        ga = gather(T.lo, 8 * ds[0], len(ds), [tl], 4 * z)
        if ds[-1] == 3:
            claims()
        q = do("v", ga, lambda e: e.quantize_mx(T.hq[:, z:z + n], T.hp[:, z:z + n], T.h[:, 4 * z:4 * (z + n)]))
        for d in ds:
            if d not in O["via"]:
                send_tiles([q], [], [back(Y[d], off, T.hq, T.hp, 128 * d - 128)])
        send_tiles([q], [], [(lanes[d], T.hq, T.hp, 128 * d - 128, 128, [(helper[d], T.crq, T.crp, 256)], "cl", "clp") for d in O["via"]])

    far = [a for a in range(N) if a != me]
    parts = sorted(far, key=lambda a: road(a, me, O["arr"]))
    for a in parts[:O["early"]]:
        decode2(a)
    near = [q_own, ("cd4", 2 * NO), ("cd5", 2 * NO), ("cd6", 2 * NO)]
    for a, n in O["rounds"]:
        z, i = 384 + 128 * a, a // 2
        ga = gather(T.lst, 8 * a, n, [("l%d" % i, NO)], 4 * z)
        q = do("v", ga, lambda e: e.quantize_mx(T.hq[:, z:z + 128 * n], T.hp[:, z:z + 128 * n], T.h[:, 4 * z:4 * z + 512 * n]))
        send_tiles([q], [], [(e, T.hq, T.hp, z + 128 * j, 128, [(S[(a + j) % 2], T.crq, T.crp, 128 * i)], "cr%d" % i, "crp%d" % i) for j, e in enumerate(share(onchip, n))])
    load("y", "dout", T.no[0:1, :], T.won[:, 1:2], [("wl", NO)])
    load("y", "dout", T.no[2:3, :], T.won[:, 0:1])

    nl = len(parts) - O["late"]
    rest = parts[O["early"]:nl]
    for step in O["seq"]:
        if step == "p":
            decode2(rest.pop(0))
        if step == "q":
            decode2(parts[nl + 1], O["l0"])
        if step == "r":
            decode2(parts[nl], O["k0"])
        if step == "n":
            decode1(4, 4, near)
        if step == "a":
            decode1(0, 2, [("cd0", 2 * NO), ("cd1", 2 * NO)])
        if step == "b":
            decode1(2, 2, [("cd2", 2 * NO), ("cd3", 2 * NO)])
        if step in "0123":
            decode1(int(step), 1, [("cd" + step, 2 * NO)])
    assert not rest
    for t in range(4):
        k = do("v", [("wl", NO)] + k_w1, lambda e: e.tensor_tensor(T.rb[:, t:512:4], T.dw1[:, 1024 * t:1024 * t + 1024].indirect(T.lst[:, 32:40]), T.xb[:, t:512:4], ADD))
    q_r = do("v", [k], lambda e: e.quantize_mx(T.rq[:, :], T.rp[:, :], T.rb[:, :]))
    decode2(parts[nl], O["k1"])
    decode2(parts[nl + 1], O["l1"])

    n = O["run"]
    n2 = NK // n
    n1 = n2 - 1
    cn = []
    for i in range(n2):
        z = n * i
        b, k = product([q_r] + [("c2a%d" % a, 4 * NO) for a in parts], T.rq, T.rp, 0, T.c2q, T.c2p, z, n)
        last = do("v", [k], lambda e: e.tensor_tensor_scan(T.m2[:, z:z + n], T.ps[:, 512 * b:512 * b + n], T.neg[:, 0:n], BIG, MAX, MAX))
        banks["free"][b] = [last]
        cn.append(do("s", [last], lambda e: e.activation(T.junk2[:, z:z + n], T.m2[:, z:z + n], SIGN, bias=T.m2[:, z + n - 1:z + n], scale=-1.0, accum_out=T.cnt[:, i:i + 1])))
        if i == n1:
            k = do("v", cn[:n1] + [k_o], lambda e: e.tensor_tensor(T.cnt[:, 16:16 + n1], T.cnt[:, 0:n1], T.pidx[:, 0:n1], ADD))
    ends = T.m2[:, n - 1:NK:n]
    k_m = do("v", [last], lambda e: e.tensor_reduce(T.cnt[:, 48:49], ends, AxisListType.X, MAX))
    load("y", "dout", T.no[3:4, :], T.cnt[:, 48:49], [k_m])
    k = do("v", [k_m], lambda e: e.tensor_scalar(T.cnt[:, 32:32 + n1], T.m2[:, n - 1:NK - 1:n], T.cnt[:, 48:49], 16384.0, AluOpType.is_lt, MUL))
    k = do("v", [k], lambda e: e.tensor_tensor(T.cnt[:, 52:52 + n1], T.cnt[:, 32:32 + n1], T.cnt[:, 16:16 + n1], ADD))
    k_c = do("v", [k], lambda e: e.tensor_reduce(T.cnt[:, 49:50], T.cnt[:, 52:52 + n1], AxisListType.X, MIN))
    decode2(parts[nl + 1], O["l2"])
    k = do("v", [k_c, cn[n1]], lambda e: e.tensor_scalar(T.cnt[:, 50:51], T.cnt[:, n1:n2], float(n * n1), T.cnt[:, 49:50], ADD, MIN))
    load("y", "dout", T.no[1:2, :], T.cnt[:, 50:51], [k])
    k = build_lists(4, T.mask4, [T.cnt[:, 50:51]], [[k] + k4], 128, 32, False)
    for i, q in enumerate("sy"):
        f = slice(256 * i, 256 * i + 256)
        r = do("v", [k] + k_w2, lambda e: e.tensor_tensor(T.yo[:, f], T.dw2[:, :].indirect(T.lo[:, 32 + 16 * i:48 + 16 * i]), T.rb[:, f], ADD))
        load(q, "dout", T.y[:, f], T.yo[:, f], [r])
    finish()
